import numpy as np
import ml_dtypes


def mxq(x, axis, fmt="e4m3"):
    dtype, down = {"e4m3": (ml_dtypes.float8_e4m3fn, 7), "e5m2": (ml_dtypes.float8_e5m2, 14)}[fmt]
    v = np.moveaxis(np.asarray(x, np.float32).astype(ml_dtypes.bfloat16).astype(np.float64), axis, -1)
    blocks = v.reshape(v.shape[:-1] + (-1, 32))
    amax = np.abs(blocks).max(-1, keepdims=True)
    byte = np.maximum(np.where(amax > 0, np.frexp(amax)[1] - 1 + 127, 0) - down, 1)
    scale = np.exp2(byte - 127.0)
    codes = (blocks / scale).astype(np.float32).astype(dtype).astype(np.float64)
    return np.moveaxis((codes * scale).reshape(v.shape), -1, axis)


WIDE = False


def mx_kscale(k):
    if not WIDE:
        return np.ones(k)
    levels = np.array([30, -30])
    if k % 512:
        return np.exp2(np.random.permutation(np.resize(levels, k // 32))).repeat(32)
    a = np.empty((k // 512, 16))
    for p in range(k // 512):
        a[p, :8] = np.random.permutation(np.resize(levels, 8))
        for g in range(8):
            far = levels[np.abs(levels - a[p, g]) >= 10]
            a[p, g + 8] = far[np.random.randint(len(far))]
    return np.exp2(a.ravel()).repeat(32)


def f64(x):
    return np.asarray(x).astype(np.float64)


def striped(idx):
    return np.tile(idx.reshape(-1, 16).T, (8, 1)).astype(np.uint16)


def unstriped(offs):
    return offs[:16].T.reshape(-1).astype(np.int64)


def bf(x):
    return np.asarray(x, np.float32).astype(ml_dtypes.bfloat16)


E2M1 = np.array([0.0, 0.5, 1.0, 1.5, 2.0, 3.0, 4.0, 6.0, -0.0, -0.5, -1.0, -1.5, -2.0, -3.0, -4.0, -6.0])


def pack_weight(w, fmt):
    k, n = w.shape
    w = f64(bf(w)).reshape(k // 32, 32, n)
    amax = np.abs(w).max(1)
    if fmt in ("e4m3", "e5m2"):
        byte = np.frexp(amax)[1] - 1 + 127 - (7 if fmt == "e4m3" else 14)
    else:
        mant, ex = np.frexp(amax / 6.0)
        byte = np.where(mant > 0.5, ex, ex - 1) + 127
    byte = np.clip(np.where(amax > 0, byte, 1), 1, 254)
    scaled = (w * np.exp2(127.0 - byte)[:, None, :]).reshape(k, n).astype(np.float32)
    by_word = np.ascontiguousarray(scaled.reshape(k // 512, 128, 4, n).transpose(0, 1, 3, 2))
    if fmt in ("e4m3", "e5m2"):
        words = by_word.astype(ml_dtypes.float8_e4m3fn if fmt == "e4m3" else ml_dtypes.float8_e5m2).view(np.uint8)
    else:
        c = by_word.astype(ml_dtypes.float4_e2m1fn).view(np.uint8) & 0xF
        words = c[..., 0::2] | (c[..., 1::2] << 4)
    return np.ascontiguousarray(words), np.ascontiguousarray(byte.astype(np.uint8).reshape(k // 512, 16, n))


def unpack_weight(words, scales, fmt):
    g, p, n, _ = words.shape
    if fmt in ("e4m3", "e5m2"):
        vals = np.ascontiguousarray(words).view(ml_dtypes.float8_e4m3fn if fmt == "e4m3" else ml_dtypes.float8_e5m2).astype(np.float64)
    else:
        nib = np.empty((g, p, n, 4), np.uint8)
        nib[..., 0::2] = words & 0xF
        nib[..., 1::2] = words >> 4
        vals = E2M1[nib]
    vals = vals * np.repeat(np.exp2(scales.astype(np.float64) - 127.0), 8, axis=1)[..., None]
    return vals.transpose(0, 1, 3, 2).reshape(g * 512, n)


K, H, N, T, S, T2 = 1024, 512, 1024, 2048, 1024, 2048

def setup_inputs():
    n = np.random.standard_normal
    s = mx_kscale(K)[:, None]
    u = mx_kscale(H)[:, None]
    v = n((K, T)) * np.exp(1.0 * n((1, T))) * s
    tab_words, tab_scales = pack_weight(v, "e5m2")
    c = -0.6 * n((K, N)) / np.sqrt(K) / s / s.T
    c_words, c_scales = pack_weight(c, "e4m3")
    return {
        "tab_words": tab_words, "tab_scales": tab_scales,
        "offs": striped(np.random.permutation(T)[:S]),
        "offs2": striped(np.random.permutation(T2)[:S]),
        "sT": np.tanh(n((H, T))).astype(np.float32),
        "w": (n((K, H)) / np.sqrt(K) / s * u.T).astype(np.float32),
        "slope": (1.5 * np.exp(0.3 * n(H)) / u[:, 0] ** 2).astype(np.float32),
        "c_words": c_words, "c_scales": c_scales,
        "gain": (np.exp(0.3 * n(N)) * s[:, 0]).astype(np.float32),
        "wgo": np.exp(0.3 * n((128, S))).astype(np.float32),
    }

def reference(tab_words, tab_scales, offs, offs2, sT, w, slope, c_words, c_scales, gain, wgo):
    v = unpack_weight(tab_words, tab_scales, "e5m2")[:, unstriped(offs)]
    c = unpack_weight(c_words, c_scales, "e4m3")
    s_ = f64(sT)[:, unstriped(offs)]
    h = mxq(f64(w), 0, "e4m3").T @ v
    d = f64(slope)[:, None] * (h * ((1 - s_) * (1 + s_)))
    dq = mxq(d, 0, "e4m3")
    x = mxq(f64(w).T, 0, "e4m3").T @ dq + c.T @ v
    y = f64(gain)[:, None] * x
    out = np.zeros((N, T2))
    out[:, unstriped(offs2)] = np.tile(f64(wgo), (N // 128, 1)) * y
    return out

@@ -1,0 +1,251 @@
+from contextlib import ExitStack
+
+import concourse.mybir as mybir
+from concourse.masks import make_identity
+
+K, H, N, T, S = 1024, 512, 1024, 2048, 1024
+FLOPS = 2 * S * (K * H + H * N + K * N)
+
+F32 = mybir.dt.float32
+BF16 = mybir.dt.bfloat16
+I32 = mybir.dt.int32
+U32 = mybir.dt.uint32
+U16 = mybir.dt.uint16
+U8 = mybir.dt.uint8
+E4M3 = mybir.dt.float8_e4m3fn_x4
+E5M2 = mybir.dt.float8_e5m2_x4
+MULT = mybir.AluOpType.mult
+COPY = mybir.ActivationFunctionType.Copy
+SQUARE = mybir.ActivationFunctionType.Square
+
+P = 128
+PACK = 4
+PASS = P * PACK
+HALF = 512
+PAGES = 3
+
+
+def tile_list_tied_jet_gradient_kernel(
+    tc, tab_words, tab_scales, offs, offs2, sT, w, slope, c_words, c_scales, gain, wgo, out
+):
+    nc = tc.nc
+    with ExitStack() as ctx:
+        keep = ctx.enter_context(tc.tile_pool(name="keep", bufs=1))
+        ring = ctx.enter_context(tc.tile_pool(name="ring", bufs=2))
+        yring = ctx.enter_context(tc.tile_pool(name="yring", bufs=3))
+        ps_turn = ctx.enter_context(tc.psum_pool(name="ps_turn", bufs=2))
+        ps_h = ctx.enter_context(tc.psum_pool(name="ps_h", bufs=4))
+        ps_y = ctx.enter_context(tc.psum_pool(name="ps_y", bufs=2))
+
+        def held(name, shape, dtype):
+            return keep.tile(shape, dtype, name=name, align_bytes=64)
+
+        idx = keep.tile([P, S // 16], U16, name="idx")
+        idx2 = keep.tile([P, S // 16], U16, name="idx2")
+        tab_w = [held("tab_w%d" % a, [P, T], U32) for a in range(2)]
+        tab_s = held("tab_s", [P, T], U8)
+        v_w = [held("v_w%d" % a, [P, S], U32) for a in range(2)]
+        v_s = [held("v_s%d" % a, [P, S], U8) for a in range(2)]
+        w_raw = [held("w_raw%d" % a, [P, PACK, H], F32) for a in range(2)]
+        wk_in = [held("wk_in%d" % a, [P, PACK * H], BF16) for a in range(2)]
+        wk_w = [held("wk_w%d" % a, [P, H], U32) for a in range(2)]
+        wk_s = [held("wk_s%d" % a, [P, H], U8) for a in range(2)]
+        wr_in = [held("wr_in%d" % a, [P, PACK * PASS], BF16) for a in range(2)]
+        wr_w = [held("wr_w%d" % a, [P, PASS], U32) for a in range(2)]
+        wr_s = [held("wr_s%d" % a, [P, PASS], U8) for a in range(2)]
+        s_raw = [held("s_raw%d" % t, [P, T], F32) for t in range(PACK)]
+        s_pick = [held("s_pick%d" % t, [P, S], F32) for t in range(PACK)]
+        d_rows = [held("d_rows%d" % f, [P, PACK, HALF], BF16) for f in range(2)]
+        d_in = [held("d_in%d" % f, [P, PACK * HALF], BF16) for f in range(2)]
+        d_w = [held("d_w%d" % f, [P, HALF], U32) for f in range(2)]
+        d_s = [held("d_s%d" % f, [P, HALF], U8) for f in range(2)]
+        c_w = [held("c_w%d" % a, [P, N], U32) for a in range(2)]
+        c_s = held("c_s", [P, 2, N], U8)
+        slope_sb = held("slope_sb", [P, PACK], F32)
+        gain_rows = held("gain_rows", [P, P], F32)
+        gain_sb = held("gain_sb", [P, N // P], F32)
+        wgo_sb = held("wgo_sb", [P, S], F32)
+        ident = held("ident", [P, P], F32)
+        pages = [held("page%d" % g, [P, T], F32) for g in range(PAGES)]
+
+        def cols(f):
+            return slice(f * HALF, (f + 1) * HALF)
+
+        def entries(f):
+            return slice(f * HALF // 16, (f + 1) * HALF // 16)
+
+        nc.vector.memset(tab_s[:].bitcast(I32), 0)
+        nc.vector.memset(v_s[1][:].bitcast(I32), 0)
+        nc.vector.memset(c_s[:].bitcast(I32), 0)
+        for page in pages:
+            nc.vector.memset(page[:], 0.0)
+        nc.gpsimd.memset(gain_rows[:], 0.0)
+        make_identity(nc, ident[:])
+
+        def load_words(tile, words):
+            nc.sync.dma_start(out=tile[:].bitcast(I32), in_=words.rearrange("p t i -> p (t i)").bitcast(I32))
+
+        def load_w(a):
+            nc.sync.dma_start(out=w_raw[a][:], in_=w[PASS * a : PASS * (a + 1), :].rearrange("(p i) r -> p i r", i=PACK))
+
+        def load_s(t):
+            nc.sync.dma_start(out=s_raw[t][:], in_=sT.rearrange("(p t) x -> p t x", t=PACK)[:, t, :])
+
+        nc.sync.dma_start(idx[:], offs)
+        load_words(tab_w[0], tab_words[0])
+        for q in range(4):
+            nc.sync.dma_start(
+                out=tab_s[32 * q : 32 * q + 8, :].bitcast(I32), in_=tab_scales.bitcast(I32)[:, 4 * q : 4 * q + 4, :]
+            )
+        load_w(0)
+        load_words(tab_w[1], tab_words[1])
+        load_s(0)
+        load_w(1)
+        nc.sync.dma_start(out=slope_sb[:], in_=slope.rearrange("(p t) -> p t", t=PACK))
+        load_s(1)
+        load_s(2)
+        load_s(3)
+        for q in range(4):
+            nc.sync.dma_start(
+                out=c_s[32 * q : 32 * q + 4, :, :].bitcast(I32),
+                in_=c_scales.bitcast(I32)[:, 4 * q : 4 * q + 4, :].rearrange("a q n -> q a n"),
+            )
+        nc.sync.dma_start(out=gain_rows[0 : N // P, :], in_=gain.rearrange("(b p) -> b p", p=P))
+        nc.sync.dma_start(idx2[:], offs2)
+        load_words(c_w[0], c_words[0])
+        load_words(c_w[1], c_words[1])
+        nc.sync.dma_start(out=wgo_sb[:], in_=wgo)
+
+        def pick_words(a):
+            nc.vector.tensor_copy(v_w[a][:], tab_w[a][:].indirect(idx[:]))
+
+        def pick_scales():
+            nc.vector.tensor_copy(v_s[0][:], tab_s[:].indirect(idx[:]))
+            nc.scalar.dma_start(out=v_s[1][0:112, :].bitcast(I32), in_=v_s[0][4:116, :].bitcast(I32))
+
+        def quantise(words, scales, values):
+            nc.vector.quantize_mx(out=words[:].bitcast(E4M3), scales=scales[:], in_=values[:])
+
+        def lay_w(a):
+            nc.scalar.copy(
+                out=wk_in[a][:].rearrange("p (t m i) -> p m t i", t=PACK, i=PACK),
+                in_=w_raw[a][:].rearrange("p i (m t) -> p m t i", t=PACK),
+            )
+
+        def turn_w(a):
+            pairs = wk_in[a][:].bitcast(F32)
+            for u in range(2):
+                bank = ps_turn.tile([P, PACK * P], F32, name="turn")
+                for t in range(PACK):
+                    nc.tensor.transpose(
+                        bank[:, P * t : P * (t + 1)], pairs[:, 2 * P * t + u : 2 * P * (t + 1) : 2], ident[:]
+                    )
+                nc.scalar.copy(
+                    out=wr_in[a][:].rearrange("m (p u e t) -> m u p e t", u=2, e=2, t=PACK)[:, u],
+                    in_=bank[:].bitcast(BF16).rearrange("m (t p e) -> m p e t", t=PACK, e=2),
+                )
+
+        def pick_s(t, part, ent):
+            nc.vector.tensor_copy(s_pick[t][:, part], s_raw[t][:].indirect(idx[:, ent]))
+            square = ring.tile([P, S], F32, name="square")
+            nc.scalar.activation(square[:, part], s_pick[t][:, part], SQUARE)
+            nc.scalar.activation(s_pick[t][:, part], square[:, part], COPY, bias=1.0, scale=-1.0)
+
+        def make_d(t, f):
+            h = ps_h.tile([P, HALF], F32, name="h")
+            for a in range(2):
+                nc.tensor.matmul_mx(
+                    out=h[:],
+                    lhsT=wk_w[a][:, P * t : P * (t + 1)].bitcast(E4M3),
+                    lhsT_scale=wk_s[a][:, P * t : P * (t + 1)],
+                    rhs=v_w[a][:, cols(f)].bitcast(E5M2),
+                    rhs_scale=v_s[a][:, cols(f)],
+                    start=(a == 0),
+                    stop=(a == 1),
+                )
+            nc.vector.scalar_tensor_tensor(
+                d_rows[f][:, t, :], h[:], slope_sb[:, t : t + 1], s_pick[t][:, cols(f)], MULT, MULT
+            )
+
+        def lay_d(f):
+            nc.scalar.copy(
+                out=d_in[f][:].rearrange("p (c i t) -> p c t i", t=PACK, i=4),
+                in_=d_rows[f][:].rearrange("p t (c i) -> p c t i", i=4),
+            )
+
+        def make_y(b, f, y):
+            acc = ps_y.tile([P, HALF], F32, name="acc")
+            for a in range(2):
+                nc.tensor.matmul_mx(
+                    out=acc[:],
+                    lhsT=c_w[a][:, P * b : P * (b + 1)].bitcast(E4M3),
+                    lhsT_scale=c_s[:, a, P * b : P * (b + 1)],
+                    rhs=v_w[a][:, cols(f)].bitcast(E5M2),
+                    rhs_scale=v_s[a][:, cols(f)],
+                    start=(a == 0),
+                    stop=False,
+                )
+            a, j = divmod(b, PACK)
+            nc.tensor.matmul_mx(
+                out=acc[:],
+                lhsT=wr_w[a][:, P * j : P * (j + 1)].bitcast(E4M3),
+                lhsT_scale=wr_s[a][:, P * j : P * (j + 1)],
+                rhs=d_w[f][:].bitcast(E4M3),
+                rhs_scale=d_s[f][:],
+                start=False,
+                stop=True,
+            )
+            nc.scalar.activation(y[:, cols(f)], acc[:], COPY, scale=gain_sb[:, b : b + 1])
+
+        def place(b, y, part, ent):
+            nc.vector.tensor_tensor(pages[b % PAGES][:].indirect(idx2[:, ent]), y[:, part], wgo_sb[:, part], MULT)
+
+        def store(b):
+            nc.sync.dma_start(out=out[P * b : P * (b + 1), :], in_=pages[b % PAGES][:])
+
+        whole, all_entries = slice(0, S), slice(0, S // 16)
+
+        pick_words(0)
+        pick_scales()
+        lay_w(0)
+        turn_w(0)
+        pick_words(1)
+        pick_s(0, whole, all_entries)
+        quantise(wk_w[0], wk_s[0], wk_in[0])
+        quantise(wr_w[0], wr_s[0], wr_in[0])
+        lay_w(1)
+        pick_s(1, whole, all_entries)
+        quantise(wk_w[1], wk_s[1], wk_in[1])
+        turn_w(1)
+        gain_bank = ps_turn.tile([P, PACK * P], F32, name="turn")
+        nc.tensor.transpose(gain_bank[:, 0:P], gain_rows[:], ident[:])
+        nc.scalar.copy(out=gain_sb[:], in_=gain_bank[:, 0 : N // P])
+        pick_s(2, whole, all_entries)
+        make_d(0, 0)
+        make_d(1, 0)
+        quantise(wr_w[1], wr_s[1], wr_in[1])
+        pick_s(3, cols(0), entries(0))
+        make_d(2, 0)
+        pick_s(3, cols(1), entries(1))
+        make_d(3, 0)
+        lay_d(0)
+        for t in range(PACK):
+            make_d(t, 1)
+        quantise(d_w[0], d_s[0], d_in[0])
+        lay_d(1)
+        first = [yring.tile([P, S], F32, name="y") for b in range(2)]
+        for b in range(2):
+            make_y(b, 0, first[b])
+            place(b, first[b], cols(0), entries(0))
+            if b == 0:
+                quantise(d_w[1], d_s[1], d_in[1])
+        for b in range(2):
+            make_y(b, 1, first[b])
+            place(b, first[b], cols(1), entries(1))
+            store(b)
+        for b in range(2, N // P):
+            y = yring.tile([P, S], F32, name="y")
+            for f in range(2):
+                make_y(b, f, y)
+            place(b, y, whole, all_entries)
+            store(b)

@@ -33,9 +33,8 @@ def tile_list_tied_jet_gradient_kernel(
         keep = ctx.enter_context(tc.tile_pool(name="keep", bufs=1))
         ring = ctx.enter_context(tc.tile_pool(name="ring", bufs=2))
         yring = ctx.enter_context(tc.tile_pool(name="yring", bufs=3))
-        ps_turn = ctx.enter_context(tc.psum_pool(name="ps_turn", bufs=2))
         ps_h = ctx.enter_context(tc.psum_pool(name="ps_h", bufs=4))
-        ps_y = ctx.enter_context(tc.psum_pool(name="ps_y", bufs=2))
+        ps_y = ctx.enter_context(tc.psum_pool(name="ps_y", bufs=4))
 
         def held(name, shape, dtype):
             return keep.tile(shape, dtype, name=name, align_bytes=64)
@@ -54,8 +53,9 @@ def tile_list_tied_jet_gradient_kernel(
         wr_w = [held("wr_w%d" % a, [P, PASS], U32) for a in range(2)]
         wr_s = [held("wr_s%d" % a, [P, PASS], U8) for a in range(2)]
         s_raw = [held("s_raw%d" % t, [P, T], F32) for t in range(PACK)]
-        s_pick = [held("s_pick%d" % t, [P, S], F32) for t in range(PACK)]
-        d_rows = [held("d_rows%d" % f, [P, PACK, HALF], BF16) for f in range(2)]
+        s_pick = [held("s_pick%d" % t, [P, S], F32) for t in range(PACK - 1)]
+        s_last = [held("shared", [P, HALF], F32), held("s_last1", [P, HALF], F32)]
+        d_rows = [held("d_rows0", [P, PACK, HALF], BF16)]
         d_in = [held("d_in%d" % f, [P, PACK * HALF], BF16) for f in range(2)]
         d_w = [held("d_w%d" % f, [P, HALF], U32) for f in range(2)]
         d_s = [held("d_s%d" % f, [P, HALF], U8) for f in range(2)]
@@ -75,12 +75,12 @@ def tile_list_tied_jet_gradient_kernel(
             return slice(f * HALF // 16, (f + 1) * HALF // 16)
 
         nc.vector.memset(tab_s[:].bitcast(I32), 0)
-        nc.vector.memset(v_s[1][:].bitcast(I32), 0)
-        nc.vector.memset(c_s[:].bitcast(I32), 0)
-        for page in pages:
-            nc.vector.memset(page[:], 0.0)
-        nc.gpsimd.memset(gain_rows[:], 0.0)
         make_identity(nc, ident[:])
+        nc.gpsimd.memset(v_s[1][:].bitcast(I32), 0)
+        nc.gpsimd.memset(c_s[:].bitcast(I32), 0)
+        nc.gpsimd.memset(gain_rows[:], 0.0)
+        for page in pages:
+            nc.gpsimd.memset(page[:], 0.0)
 
         def load_words(tile, words):
             nc.sync.dma_start(out=tile[:].bitcast(I32), in_=words.rearrange("p t i -> p (t i)").bitcast(I32))
@@ -92,16 +92,16 @@ def tile_list_tied_jet_gradient_kernel(
             nc.sync.dma_start(out=s_raw[t][:], in_=sT.rearrange("(p t) x -> p t x", t=PACK)[:, t, :])
 
         nc.sync.dma_start(idx[:], offs)
-        load_words(tab_w[0], tab_words[0])
+        nc.sync.dma_start(out=slope_sb[:], in_=slope.rearrange("(p t) -> p t", t=PACK))
         for q in range(4):
             nc.sync.dma_start(
                 out=tab_s[32 * q : 32 * q + 8, :].bitcast(I32), in_=tab_scales.bitcast(I32)[:, 4 * q : 4 * q + 4, :]
             )
         load_w(0)
+        load_words(tab_w[0], tab_words[0])
+        load_w(1)
         load_words(tab_w[1], tab_words[1])
         load_s(0)
-        load_w(1)
-        nc.sync.dma_start(out=slope_sb[:], in_=slope.rearrange("(p t) -> p t", t=PACK))
         load_s(1)
         load_s(2)
         load_s(3)
@@ -121,7 +121,7 @@ def tile_list_tied_jet_gradient_kernel(
 
         def pick_scales():
             nc.vector.tensor_copy(v_s[0][:], tab_s[:].indirect(idx[:]))
-            nc.scalar.dma_start(out=v_s[1][0:112, :].bitcast(I32), in_=v_s[0][4:116, :].bitcast(I32))
+            nc.gpsimd.dma_start(out=v_s[1][0:112, :].bitcast(I32), in_=v_s[0][4:116, :].bitcast(I32))
 
         def quantise(words, scales, values):
             nc.vector.quantize_mx(out=words[:].bitcast(E4M3), scales=scales[:], in_=values[:])
@@ -135,7 +135,7 @@ def tile_list_tied_jet_gradient_kernel(
         def turn_w(a):
             pairs = wk_in[a][:].bitcast(F32)
             for u in range(2):
-                bank = ps_turn.tile([P, PACK * P], F32, name="turn")
+                bank = ps_y.tile([P, HALF], F32, name="acc")
                 for t in range(PACK):
                     nc.tensor.transpose(
                         bank[:, P * t : P * (t + 1)], pairs[:, 2 * P * t + u : 2 * P * (t + 1) : 2], ident[:]
@@ -145,11 +145,11 @@ def tile_list_tied_jet_gradient_kernel(
                     in_=bank[:].bitcast(BF16).rearrange("m (t p e) -> m p e t", t=PACK, e=2),
                 )
 
-        def pick_s(t, part, ent):
-            nc.vector.tensor_copy(s_pick[t][:, part], s_raw[t][:].indirect(idx[:, ent]))
-            square = ring.tile([P, S], F32, name="square")
-            nc.scalar.activation(square[:, part], s_pick[t][:, part], SQUARE)
-            nc.scalar.activation(s_pick[t][:, part], square[:, part], COPY, bias=1.0, scale=-1.0)
+        def pick_s(t, picked, ent):
+            nc.vector.tensor_copy(picked[:], s_raw[t][:].indirect(idx[:, ent]))
+            square = ring.tile([P, 16 * (ent.stop - ent.start)], F32, name="square")
+            nc.scalar.activation(square[:], picked[:], SQUARE)
+            nc.scalar.activation(picked[:], square[:], COPY, bias=1.0, scale=-1.0)
 
         def make_d(t, f):
             h = ps_h.tile([P, HALF], F32, name="h")
@@ -163,12 +163,11 @@ def tile_list_tied_jet_gradient_kernel(
                     start=(a == 0),
                     stop=(a == 1),
                 )
-            nc.vector.scalar_tensor_tensor(
-                d_rows[f][:, t, :], h[:], slope_sb[:, t : t + 1], s_pick[t][:, cols(f)], MULT, MULT
-            )
+            factor = s_last[f][:] if t == PACK - 1 else s_pick[t][:, cols(f)]
+            nc.vector.scalar_tensor_tensor(d_rows[f][:, t, :], h[:], slope_sb[:, t : t + 1], factor, MULT, MULT)
 
-        def lay_d(f):
-            nc.scalar.copy(
+        def lay_d(f, copy):
+            copy(
                 out=d_in[f][:].rearrange("p (c i t) -> p c t i", t=PACK, i=4),
                 in_=d_rows[f][:].rearrange("p t (c i) -> p c t i", i=4),
             )
@@ -205,44 +204,44 @@ def tile_list_tied_jet_gradient_kernel(
 
         whole, all_entries = slice(0, S), slice(0, S // 16)
 
-        pick_words(0)
         pick_scales()
         lay_w(0)
-        turn_w(0)
-        pick_words(1)
-        pick_s(0, whole, all_entries)
-        quantise(wk_w[0], wk_s[0], wk_in[0])
-        quantise(wr_w[0], wr_s[0], wr_in[0])
+        pick_words(0)
         lay_w(1)
-        pick_s(1, whole, all_entries)
+        turn_w(0)
+        quantise(wk_w[0], wk_s[0], wk_in[0])
+        pick_words(1)
         quantise(wk_w[1], wk_s[1], wk_in[1])
-        turn_w(1)
-        gain_bank = ps_turn.tile([P, PACK * P], F32, name="turn")
-        nc.tensor.transpose(gain_bank[:, 0:P], gain_rows[:], ident[:])
-        nc.scalar.copy(out=gain_sb[:], in_=gain_bank[:, 0 : N // P])
-        pick_s(2, whole, all_entries)
+        pick_s(0, s_pick[0], all_entries)
+        quantise(wr_w[0], wr_s[0], wr_in[0])
+        pick_s(1, s_pick[1], all_entries)
+        pick_s(2, s_pick[2], all_entries)
         make_d(0, 0)
         make_d(1, 0)
-        quantise(wr_w[1], wr_s[1], wr_in[1])
-        pick_s(3, cols(0), entries(0))
+        pick_s(3, s_last[0], entries(0))
         make_d(2, 0)
-        pick_s(3, cols(1), entries(1))
+        pick_s(3, s_last[1], entries(1))
+        gain_bank = ps_y.tile([P, HALF], F32, name="acc")
+        nc.tensor.transpose(gain_bank[:, 0:P], gain_rows[:], ident[:])
+        nc.scalar.copy(out=gain_sb[:], in_=gain_bank[:, 0 : N // P])
         make_d(3, 0)
-        lay_d(0)
+        lay_d(0, nc.scalar.copy)
+        d_rows.append(held("shared", [P, PACK, HALF], BF16))
         for t in range(PACK):
             make_d(t, 1)
         quantise(d_w[0], d_s[0], d_in[0])
-        lay_d(1)
+        lay_d(1, nc.vector.tensor_copy)
+        quantise(d_w[1], d_s[1], d_in[1])
         first = [yring.tile([P, S], F32, name="y") for b in range(2)]
         for b in range(2):
             make_y(b, 0, first[b])
             place(b, first[b], cols(0), entries(0))
-            if b == 0:
-                quantise(d_w[1], d_s[1], d_in[1])
         for b in range(2):
             make_y(b, 1, first[b])
             place(b, first[b], cols(1), entries(1))
             store(b)
+        turn_w(1)
+        quantise(wr_w[1], wr_s[1], wr_in[1])
         for b in range(2, N // P):
             y = yring.tile([P, S], F32, name="y")
             for f in range(2):

@@ -66,7 +66,7 @@ def tile_list_tied_jet_gradient_kernel(
         gain_sb = held("gain_sb", [P, N // P], F32)
         wgo_sb = held("wgo_sb", [P, S], F32)
         ident = held("ident", [P, P], F32)
-        pages = [held("page%d" % g, [P, T], F32) for g in range(PAGES)]
+        pages = [held("page%d" % g, [P, T], F32) for g in range(PAGES - 1)]
 
         def cols(f):
             return slice(f * HALF, (f + 1) * HALF)
@@ -74,13 +74,13 @@ def tile_list_tied_jet_gradient_kernel(
         def entries(f):
             return slice(f * HALF // 16, (f + 1) * HALF // 16)
 
-        nc.vector.memset(tab_s[:].bitcast(I32), 0)
-        make_identity(nc, ident[:])
+        nc.gpsimd.memset(tab_s[:].bitcast(I32), 0)
         nc.gpsimd.memset(v_s[1][:].bitcast(I32), 0)
+        make_identity(nc, ident[:])
         nc.gpsimd.memset(c_s[:].bitcast(I32), 0)
         nc.gpsimd.memset(gain_rows[:], 0.0)
         for page in pages:
-            nc.gpsimd.memset(page[:], 0.0)
+            nc.vector.memset(page[:], 0.0)
 
         def load_words(tile, words):
             nc.sync.dma_start(out=tile[:].bitcast(I32), in_=words.rearrange("p t i -> p (t i)").bitcast(I32))
@@ -92,15 +92,16 @@ def tile_list_tied_jet_gradient_kernel(
             nc.sync.dma_start(out=s_raw[t][:], in_=sT.rearrange("(p t) x -> p t x", t=PACK)[:, t, :])
 
         nc.sync.dma_start(idx[:], offs)
-        nc.sync.dma_start(out=slope_sb[:], in_=slope.rearrange("(p t) -> p t", t=PACK))
-        for q in range(4):
+        for r in range(4):
             nc.sync.dma_start(
-                out=tab_s[32 * q : 32 * q + 8, :].bitcast(I32), in_=tab_scales.bitcast(I32)[:, 4 * q : 4 * q + 4, :]
+                out=tab_s[r:P:16, :].bitcast(I32),
+                in_=tab_scales.bitcast(I32)[:, r:16:4, :].rearrange("a q n -> q a n"),
             )
         load_w(0)
         load_words(tab_w[0], tab_words[0])
         load_w(1)
         load_words(tab_w[1], tab_words[1])
+        nc.sync.dma_start(out=slope_sb[:], in_=slope.rearrange("(p t) -> p t", t=PACK))
         load_s(0)
         load_s(1)
         load_s(2)
@@ -121,7 +122,7 @@ def tile_list_tied_jet_gradient_kernel(
 
         def pick_scales():
             nc.vector.tensor_copy(v_s[0][:], tab_s[:].indirect(idx[:]))
-            nc.gpsimd.dma_start(out=v_s[1][0:112, :].bitcast(I32), in_=v_s[0][4:116, :].bitcast(I32))
+            nc.gpsimd.dma_start(out=v_s[1][0:112, :].bitcast(I32), in_=v_s[0][16:128, :].bitcast(I32))
 
         def quantise(words, scales, values):
             nc.vector.quantize_mx(out=words[:].bitcast(E4M3), scales=scales[:], in_=values[:])
@@ -232,6 +233,8 @@ def tile_list_tied_jet_gradient_kernel(
         quantise(d_w[0], d_s[0], d_in[0])
         lay_d(1, nc.vector.tensor_copy)
         quantise(d_w[1], d_s[1], d_in[1])
+        pages.append(held("d_in1", [P, T], F32))
+        nc.gpsimd.memset(pages[-1][:], 0.0)
         first = [yring.tile([P, S], F32, name="y") for b in range(2)]
         for b in range(2):
             make_y(b, 0, first[b])

@@ -91,13 +91,13 @@ def tile_list_tied_jet_gradient_kernel(
         def load_s(t):
             nc.sync.dma_start(out=s_raw[t][:], in_=sT.rearrange("(p t) x -> p t x", t=PACK)[:, t, :])
 
+        load_w(0)
         nc.sync.dma_start(idx[:], offs)
         for r in range(4):
             nc.sync.dma_start(
                 out=tab_s[r:P:16, :].bitcast(I32),
                 in_=tab_scales.bitcast(I32)[:, r:16:4, :].rearrange("a q n -> q a n"),
             )
-        load_w(0)
         load_words(tab_w[0], tab_words[0])
         load_w(1)
         load_words(tab_w[1], tab_words[1])

@@ -15,6 +15,7 @@ U8 = mybir.dt.uint8
 E4M3 = mybir.dt.float8_e4m3fn_x4
 E5M2 = mybir.dt.float8_e5m2_x4
 MULT = mybir.AluOpType.mult
+ADD = mybir.AluOpType.add
 COPY = mybir.ActivationFunctionType.Copy
 SQUARE = mybir.ActivationFunctionType.Square
 
@@ -23,6 +24,7 @@ PACK = 4
 PASS = P * PACK
 HALF = 512
 PAGES = 3
+ON_GPSIMD = 2
 
 
 def tile_list_tied_jet_gradient_kernel(
@@ -31,7 +33,6 @@ def tile_list_tied_jet_gradient_kernel(
     nc = tc.nc
     with ExitStack() as ctx:
         keep = ctx.enter_context(tc.tile_pool(name="keep", bufs=1))
-        ring = ctx.enter_context(tc.tile_pool(name="ring", bufs=2))
         yring = ctx.enter_context(tc.tile_pool(name="yring", bufs=3))
         ps_h = ctx.enter_context(tc.psum_pool(name="ps_h", bufs=4))
         ps_y = ctx.enter_context(tc.psum_pool(name="ps_y", bufs=4))
@@ -53,10 +54,13 @@ def tile_list_tied_jet_gradient_kernel(
         wr_w = [held("wr_w%d" % a, [P, PASS], U32) for a in range(2)]
         wr_s = [held("wr_s%d" % a, [P, PASS], U8) for a in range(2)]
         s_raw = [held("s_raw%d" % t, [P, T], F32) for t in range(PACK)]
-        s_pick = [held("s_pick%d" % t, [P, S], F32) for t in range(PACK - 1)]
-        s_last = [held("shared", [P, HALF], F32), held("s_last1", [P, HALF], F32)]
-        d_rows = [held("d_rows0", [P, PACK, HALF], BF16)]
-        d_in = [held("d_in%d" % f, [P, PACK * HALF], BF16) for f in range(2)]
+        s_pick = [[held("s_pick%d%d" % (t, f), [P, HALF], F32) for f in range(2)] for t in range(PACK)]
+        h_sb = [[held("h_sb%d%d" % (t, f), [P, HALF], F32) for f in range(2)] for t in range(ON_GPSIMD)]
+        d_first = held("d_first", [P, PACK * HALF], BF16)
+        d_both = held("d_both", [P, (PACK + ON_GPSIMD) * HALF], BF16)
+        d_last = held("d_last", [P, PACK * HALF], BF16)
+        d_rows = [d_first[:], d_both[:, 0 : PACK * HALF]]
+        d_in = [d_both[:, ON_GPSIMD * HALF :], d_last[:]]
         d_w = [held("d_w%d" % f, [P, HALF], U32) for f in range(2)]
         d_s = [held("d_s%d" % f, [P, HALF], U8) for f in range(2)]
         c_w = [held("c_w%d" % a, [P, N], U32) for a in range(2)]
@@ -75,10 +79,10 @@ def tile_list_tied_jet_gradient_kernel(
             return slice(f * HALF // 16, (f + 1) * HALF // 16)
 
         nc.gpsimd.memset(tab_s[:].bitcast(I32), 0)
+        nc.gpsimd.memset(gain_rows[:], 0.0)
         nc.gpsimd.memset(v_s[1][:].bitcast(I32), 0)
         make_identity(nc, ident[:])
         nc.gpsimd.memset(c_s[:].bitcast(I32), 0)
-        nc.gpsimd.memset(gain_rows[:], 0.0)
         for page in pages:
             nc.vector.memset(page[:], 0.0)
 
@@ -88,8 +92,8 @@ def tile_list_tied_jet_gradient_kernel(
         def load_w(a):
             nc.sync.dma_start(out=w_raw[a][:], in_=w[PASS * a : PASS * (a + 1), :].rearrange("(p i) r -> p i r", i=PACK))
 
-        def load_s(t):
-            nc.sync.dma_start(out=s_raw[t][:], in_=sT.rearrange("(p t) x -> p t x", t=PACK)[:, t, :])
+        def load_s(t, part):
+            nc.sync.dma_start(out=s_raw[t][:, part], in_=sT.rearrange("(p t) x -> p t x", t=PACK)[:, t, part])
 
         load_w(0)
         nc.sync.dma_start(idx[:], offs)
@@ -102,17 +106,17 @@ def tile_list_tied_jet_gradient_kernel(
         load_w(1)
         load_words(tab_w[1], tab_words[1])
         nc.sync.dma_start(out=slope_sb[:], in_=slope.rearrange("(p t) -> p t", t=PACK))
-        load_s(0)
-        load_s(1)
-        load_s(2)
-        load_s(3)
+        load_s(0, slice(0, T // 2))
+        load_s(0, slice(T // 2, T))
+        nc.sync.dma_start(out=gain_rows[0 : N // P, :], in_=gain.rearrange("(b p) -> b p", p=P))
+        nc.sync.dma_start(idx2[:], offs2)
+        for t in range(1, PACK):
+            load_s(t, slice(0, T))
         for q in range(4):
             nc.sync.dma_start(
                 out=c_s[32 * q : 32 * q + 4, :, :].bitcast(I32),
                 in_=c_scales.bitcast(I32)[:, 4 * q : 4 * q + 4, :].rearrange("a q n -> q a n"),
             )
-        nc.sync.dma_start(out=gain_rows[0 : N // P, :], in_=gain.rearrange("(b p) -> b p", p=P))
-        nc.sync.dma_start(idx2[:], offs2)
         load_words(c_w[0], c_words[0])
         load_words(c_w[1], c_words[1])
         nc.sync.dma_start(out=wgo_sb[:], in_=wgo)
@@ -125,7 +129,7 @@ def tile_list_tied_jet_gradient_kernel(
             nc.gpsimd.dma_start(out=v_s[1][0:112, :].bitcast(I32), in_=v_s[0][16:128, :].bitcast(I32))
 
         def quantise(words, scales, values):
-            nc.vector.quantize_mx(out=words[:].bitcast(E4M3), scales=scales[:], in_=values[:])
+            nc.vector.quantize_mx(out=words[:].bitcast(E4M3), scales=scales[:], in_=values)
 
         def lay_w(a):
             nc.scalar.copy(
@@ -146,13 +150,16 @@ def tile_list_tied_jet_gradient_kernel(
                     in_=bank[:].bitcast(BF16).rearrange("m (t p e) -> m p e t", t=PACK, e=2),
                 )
 
-        def pick_s(t, picked, ent):
-            nc.vector.tensor_copy(picked[:], s_raw[t][:].indirect(idx[:, ent]))
-            square = ring.tile([P, 16 * (ent.stop - ent.start)], F32, name="square")
-            nc.scalar.activation(square[:], picked[:], SQUARE)
-            nc.scalar.activation(picked[:], square[:], COPY, bias=1.0, scale=-1.0)
+        def pick_s(t, f):
+            picked = s_pick[t][f]
+            nc.vector.tensor_copy(picked[:], s_raw[t][:].indirect(idx[:, entries(f)]))
+            nc.scalar.activation(picked[:], picked[:], SQUARE)
+            if t < ON_GPSIMD:
+                nc.gpsimd.tensor_scalar(picked[:], picked[:], -1.0, 1.0, MULT, ADD)
+            else:
+                nc.scalar.activation(picked[:], picked[:], COPY, bias=1.0, scale=-1.0)
 
-        def make_d(t, f):
+        def make_h(t, f):
             h = ps_h.tile([P, HALF], F32, name="h")
             for a in range(2):
                 nc.tensor.matmul_mx(
@@ -164,13 +171,23 @@ def tile_list_tied_jet_gradient_kernel(
                     start=(a == 0),
                     stop=(a == 1),
                 )
-            factor = s_last[f][:] if t == PACK - 1 else s_pick[t][:, cols(f)]
-            nc.vector.scalar_tensor_tensor(d_rows[f][:, t, :], h[:], slope_sb[:, t : t + 1], factor, MULT, MULT)
+            return h
+
+        def empty_h(t, f):
+            nc.scalar.activation(h_sb[t][f][:], make_h(t, f)[:], COPY, scale=slope_sb[:, t : t + 1])
+
+        def make_d(t, f):
+            if t < ON_GPSIMD:
+                nc.gpsimd.tensor_tensor(d_rows[f][:, cols(t)], h_sb[t][f][:], s_pick[t][f][:], MULT)
+            else:
+                nc.vector.scalar_tensor_tensor(
+                    d_rows[f][:, cols(t)], make_h(t, f)[:], slope_sb[:, t : t + 1], s_pick[t][f][:], MULT, MULT
+                )
 
         def lay_d(f, copy):
             copy(
-                out=d_in[f][:].rearrange("p (c i t) -> p c t i", t=PACK, i=4),
-                in_=d_rows[f][:].rearrange("p t (c i) -> p c t i", i=4),
+                out=d_in[f].rearrange("p (c i t) -> p c t i", t=PACK, i=4),
+                in_=d_rows[f].rearrange("p (t c i) -> p c t i", t=PACK, i=4),
             )
 
         def make_y(b, f, y):
@@ -210,41 +227,43 @@ def tile_list_tied_jet_gradient_kernel(
         pick_words(0)
         lay_w(1)
         turn_w(0)
-        quantise(wk_w[0], wk_s[0], wk_in[0])
+        quantise(wk_w[0], wk_s[0], wk_in[0][:])
         pick_words(1)
-        quantise(wk_w[1], wk_s[1], wk_in[1])
-        pick_s(0, s_pick[0], all_entries)
-        quantise(wr_w[0], wr_s[0], wr_in[0])
-        pick_s(1, s_pick[1], all_entries)
-        pick_s(2, s_pick[2], all_entries)
-        make_d(0, 0)
-        make_d(1, 0)
-        pick_s(3, s_last[0], entries(0))
-        make_d(2, 0)
-        pick_s(3, s_last[1], entries(1))
+        quantise(wk_w[1], wk_s[1], wk_in[1][:])
+        quantise(wr_w[0], wr_s[0], wr_in[0][:])
+        for t in range(ON_GPSIMD):
+            for f in range(2):
+                empty_h(t, f)
+                pick_s(t, f)
+                make_d(t, f)
+        for t in range(ON_GPSIMD, PACK):
+            for f in range(2):
+                pick_s(t, f)
         gain_bank = ps_y.tile([P, HALF], F32, name="acc")
         nc.tensor.transpose(gain_bank[:, 0:P], gain_rows[:], ident[:])
         nc.scalar.copy(out=gain_sb[:], in_=gain_bank[:, 0 : N // P])
-        make_d(3, 0)
-        lay_d(0, nc.scalar.copy)
-        d_rows.append(held("shared", [P, PACK, HALF], BF16))
-        for t in range(PACK):
-            make_d(t, 1)
+        for t in range(ON_GPSIMD, PACK):
+            make_d(t, 0)
+        lay_d(0, nc.vector.tensor_copy)
         quantise(d_w[0], d_s[0], d_in[0])
-        lay_d(1, nc.vector.tensor_copy)
+        for t in range(ON_GPSIMD, PACK):
+            make_d(t, 1)
+        first = [yring.tile([P, S], F32, name="y")]
+        make_y(0, 0, first[0])
+        place(0, first[0], cols(0), entries(0))
+        lay_d(1, nc.scalar.copy)
         quantise(d_w[1], d_s[1], d_in[1])
-        pages.append(held("d_in1", [P, T], F32))
+        pages.append(held("d_last", [P, T], F32))
         nc.gpsimd.memset(pages[-1][:], 0.0)
-        first = [yring.tile([P, S], F32, name="y") for b in range(2)]
-        for b in range(2):
-            make_y(b, 0, first[b])
-            place(b, first[b], cols(0), entries(0))
+        first.append(held("d_both", [P, S], F32))
+        make_y(1, 0, first[1])
+        place(1, first[1], cols(0), entries(0))
         for b in range(2):
             make_y(b, 1, first[b])
             place(b, first[b], cols(1), entries(1))
             store(b)
         turn_w(1)
-        quantise(wr_w[1], wr_s[1], wr_in[1])
+        quantise(wr_w[1], wr_s[1], wr_in[1][:])
         for b in range(2, N // P):
             y = yring.tile([P, S], F32, name="y")
             for f in range(2):

@@ -54,7 +54,7 @@ def tile_list_tied_jet_gradient_kernel(
         wr_w = [held("wr_w%d" % a, [P, PASS], U32) for a in range(2)]
         wr_s = [held("wr_s%d" % a, [P, PASS], U8) for a in range(2)]
         s_raw = [held("s_raw%d" % t, [P, T], F32) for t in range(PACK)]
-        s_pick = [[held("s_pick%d%d" % (t, f), [P, HALF], F32) for f in range(2)] for t in range(PACK)]
+        factor = {(t, f): held("factor%d%d" % (t, f), [P, HALF], F32) for t in range(ON_GPSIMD) for f in range(2)}
         h_sb = [[held("h_sb%d%d" % (t, f), [P, HALF], F32) for f in range(2)] for t in range(ON_GPSIMD)]
         d_first = held("d_first", [P, PACK * HALF], BF16)
         d_both = held("d_both", [P, (PACK + ON_GPSIMD) * HALF], BF16)
@@ -86,8 +86,10 @@ def tile_list_tied_jet_gradient_kernel(
         for page in pages:
             nc.vector.memset(page[:], 0.0)
 
-        def load_words(tile, words):
-            nc.sync.dma_start(out=tile[:].bitcast(I32), in_=words.rearrange("p t i -> p (t i)").bitcast(I32))
+        def load_words(tile, words, part):
+            nc.sync.dma_start(
+                out=tile[:, part].bitcast(I32), in_=words.rearrange("p t i -> p (t i)").bitcast(I32)[:, part]
+            )
 
         def load_w(a):
             nc.sync.dma_start(out=w_raw[a][:], in_=w[PASS * a : PASS * (a + 1), :].rearrange("(p i) r -> p i r", i=PACK))
@@ -102,31 +104,22 @@ def tile_list_tied_jet_gradient_kernel(
                 out=tab_s[r:P:16, :].bitcast(I32),
                 in_=tab_scales.bitcast(I32)[:, r:16:4, :].rearrange("a q n -> q a n"),
             )
-        load_words(tab_w[0], tab_words[0])
+        load_words(tab_w[0], tab_words[0], slice(0, T))
         load_w(1)
-        load_words(tab_w[1], tab_words[1])
+        load_words(tab_w[1], tab_words[1], slice(0, T // 2))
+        load_words(tab_w[1], tab_words[1], slice(T // 2, T))
         nc.sync.dma_start(out=slope_sb[:], in_=slope.rearrange("(p t) -> p t", t=PACK))
-        load_s(0, slice(0, T // 2))
-        load_s(0, slice(T // 2, T))
         nc.sync.dma_start(out=gain_rows[0 : N // P, :], in_=gain.rearrange("(b p) -> b p", p=P))
         nc.sync.dma_start(idx2[:], offs2)
-        for t in range(1, PACK):
-            load_s(t, slice(0, T))
-        for q in range(4):
-            nc.sync.dma_start(
-                out=c_s[32 * q : 32 * q + 4, :, :].bitcast(I32),
-                in_=c_scales.bitcast(I32)[:, 4 * q : 4 * q + 4, :].rearrange("a q n -> q a n"),
-            )
-        load_words(c_w[0], c_words[0])
-        load_words(c_w[1], c_words[1])
-        nc.sync.dma_start(out=wgo_sb[:], in_=wgo)
+        load_s(0, slice(0, T // 2))
+        load_s(0, slice(T // 2, T))
 
         def pick_words(a):
             nc.vector.tensor_copy(v_w[a][:], tab_w[a][:].indirect(idx[:]))
 
         def pick_scales():
             nc.vector.tensor_copy(v_s[0][:], tab_s[:].indirect(idx[:]))
-            nc.gpsimd.dma_start(out=v_s[1][0:112, :].bitcast(I32), in_=v_s[0][16:128, :].bitcast(I32))
+            nc.sync.dma_start(out=v_s[1][0:112, :].bitcast(I32), in_=v_s[0][16:128, :].bitcast(I32))
 
         def quantise(words, scales, values):
             nc.vector.quantize_mx(out=words[:].bitcast(E4M3), scales=scales[:], in_=values)
@@ -150,14 +143,18 @@ def tile_list_tied_jet_gradient_kernel(
                     in_=bank[:].bitcast(BF16).rearrange("m (t p e) -> m p e t", t=PACK, e=2),
                 )
 
-        def pick_s(t, f):
-            picked = s_pick[t][f]
+        def pick_s(t, f, picked):
             nc.vector.tensor_copy(picked[:], s_raw[t][:].indirect(idx[:, entries(f)]))
-            nc.scalar.activation(picked[:], picked[:], SQUARE)
-            if t < ON_GPSIMD:
-                nc.gpsimd.tensor_scalar(picked[:], picked[:], -1.0, 1.0, MULT, ADD)
-            else:
-                nc.scalar.activation(picked[:], picked[:], COPY, bias=1.0, scale=-1.0)
+
+        def square(squared, picked):
+            nc.scalar.activation(squared[:], picked[:], SQUARE)
+
+        def one_minus(t, f, result, squared):
+            factor[t, f] = result
+            nc.scalar.activation(result[:], squared[:], COPY, bias=1.0, scale=-1.0)
+
+        def buffer(name):
+            return held(name, [P, HALF], F32)
 
         def make_h(t, f):
             h = ps_h.tile([P, HALF], F32, name="h")
@@ -178,10 +175,10 @@ def tile_list_tied_jet_gradient_kernel(
 
         def make_d(t, f):
             if t < ON_GPSIMD:
-                nc.gpsimd.tensor_tensor(d_rows[f][:, cols(t)], h_sb[t][f][:], s_pick[t][f][:], MULT)
+                nc.gpsimd.tensor_tensor(d_rows[f][:, cols(t)], h_sb[t][f][:], factor[t, f][:], MULT)
             else:
                 nc.vector.scalar_tensor_tensor(
-                    d_rows[f][:, cols(t)], make_h(t, f)[:], slope_sb[:, t : t + 1], s_pick[t][f][:], MULT, MULT
+                    d_rows[f][:, cols(t)], make_h(t, f)[:], slope_sb[:, t : t + 1], factor[t, f][:], MULT, MULT
                 )
 
         def lay_d(f, copy):
@@ -223,6 +220,16 @@ def tile_list_tied_jet_gradient_kernel(
         whole, all_entries = slice(0, S), slice(0, S // 16)
 
         pick_scales()
+        for t in range(1, PACK):
+            load_s(t, slice(0, T))
+        for q in range(4):
+            nc.sync.dma_start(
+                out=c_s[32 * q : 32 * q + 4, :, :].bitcast(I32),
+                in_=c_scales.bitcast(I32)[:, 4 * q : 4 * q + 4, :].rearrange("a q n -> q a n"),
+            )
+        load_words(c_w[0], c_words[0], slice(0, N))
+        load_words(c_w[1], c_words[1], slice(0, N))
+        nc.sync.dma_start(out=wgo_sb[:], in_=wgo)
         lay_w(0)
         pick_words(0)
         lay_w(1)
@@ -234,20 +241,34 @@ def tile_list_tied_jet_gradient_kernel(
         for t in range(ON_GPSIMD):
             for f in range(2):
                 empty_h(t, f)
-                pick_s(t, f)
+                pick_s(t, f, factor[t, f])
+                square(factor[t, f], factor[t, f])
+                nc.gpsimd.tensor_scalar(factor[t, f][:], factor[t, f][:], -1.0, 1.0, MULT, ADD)
                 make_d(t, f)
-        for t in range(ON_GPSIMD, PACK):
-            for f in range(2):
-                pick_s(t, f)
+        third, fourth, fourth_late, fourth_squared = buffer("one"), buffer("two"), buffer("three"), buffer("four")
+        pick_s(2, 0, third)
+        square(third, third)
+        pick_s(3, 0, fourth)
+        square(fourth_squared, fourth)
+        pick_s(3, 1, fourth_late)
+        one_minus(2, 0, buffer("two"), third)
+        one_minus(3, 0, fourth_squared, fourth_squared)
+        late_squared = buffer("one")
+        square(late_squared, fourth_late)
+        one_minus(3, 1, late_squared, late_squared)
         gain_bank = ps_y.tile([P, HALF], F32, name="acc")
         nc.tensor.transpose(gain_bank[:, 0:P], gain_rows[:], ident[:])
         nc.scalar.copy(out=gain_sb[:], in_=gain_bank[:, 0 : N // P])
         for t in range(ON_GPSIMD, PACK):
             make_d(t, 0)
+        third_late = buffer("two")
+        pick_s(2, 1, third_late)
+        square(third_late, third_late)
+        one_minus(2, 1, third_late, third_late)
         lay_d(0, nc.vector.tensor_copy)
         quantise(d_w[0], d_s[0], d_in[0])
-        for t in range(ON_GPSIMD, PACK):
-            make_d(t, 1)
+        make_d(3, 1)
+        make_d(2, 1)
         first = [yring.tile([P, S], F32, name="y")]
         make_y(0, 0, first[0])
         place(0, first[0], cols(0), entries(0))

@@ -54,7 +54,7 @@ def tile_list_tied_jet_gradient_kernel(
         wr_w = [held("wr_w%d" % a, [P, PASS], U32) for a in range(2)]
         wr_s = [held("wr_s%d" % a, [P, PASS], U8) for a in range(2)]
         s_raw = [held("s_raw%d" % t, [P, T], F32) for t in range(PACK)]
-        factor = {(t, f): held("factor%d%d" % (t, f), [P, HALF], F32) for t in range(ON_GPSIMD) for f in range(2)}
+        factor = {(t, f): held("factor%d%d" % (t, f), [P, HALF], F32)[:] for t in range(ON_GPSIMD) for f in range(2)}
         h_sb = [[held("h_sb%d%d" % (t, f), [P, HALF], F32) for f in range(2)] for t in range(ON_GPSIMD)]
         d_first = held("d_first", [P, PACK * HALF], BF16)
         d_both = held("d_both", [P, (PACK + ON_GPSIMD) * HALF], BF16)
@@ -143,15 +143,15 @@ def tile_list_tied_jet_gradient_kernel(
                     in_=bank[:].bitcast(BF16).rearrange("m (t p e) -> m p e t", t=PACK, e=2),
                 )
 
-        def pick_s(t, f, picked):
-            nc.vector.tensor_copy(picked[:], s_raw[t][:].indirect(idx[:, entries(f)]))
+        def pick_s(t, f, target):
+            nc.vector.tensor_copy(target, s_raw[t][:].indirect(idx[:, entries(f)]))
 
-        def square(squared, picked):
-            nc.scalar.activation(squared[:], picked[:], SQUARE)
+        def square(result, values):
+            nc.scalar.activation(result, values, SQUARE)
 
-        def one_minus(t, f, result, squared):
+        def one_minus(t, f, result, values):
             factor[t, f] = result
-            nc.scalar.activation(result[:], squared[:], COPY, bias=1.0, scale=-1.0)
+            nc.scalar.activation(result, values, COPY, bias=1.0, scale=-1.0)
 
         def buffer(name):
             return held(name, [P, HALF], F32)
@@ -175,10 +175,10 @@ def tile_list_tied_jet_gradient_kernel(
 
         def make_d(t, f):
             if t < ON_GPSIMD:
-                nc.gpsimd.tensor_tensor(d_rows[f][:, cols(t)], h_sb[t][f][:], factor[t, f][:], MULT)
+                nc.gpsimd.tensor_tensor(d_rows[f][:, cols(t)], h_sb[t][f][:], factor[t, f], MULT)
             else:
                 nc.vector.scalar_tensor_tensor(
-                    d_rows[f][:, cols(t)], make_h(t, f)[:], slope_sb[:, t : t + 1], factor[t, f][:], MULT, MULT
+                    d_rows[f][:, cols(t)], make_h(t, f)[:], slope_sb[:, t : t + 1], factor[t, f], MULT, MULT
                 )
 
         def lay_d(f, copy):
@@ -243,32 +243,28 @@ def tile_list_tied_jet_gradient_kernel(
                 empty_h(t, f)
                 pick_s(t, f, factor[t, f])
                 square(factor[t, f], factor[t, f])
-                nc.gpsimd.tensor_scalar(factor[t, f][:], factor[t, f][:], -1.0, 1.0, MULT, ADD)
+                nc.gpsimd.tensor_scalar(factor[t, f], factor[t, f], -1.0, 1.0, MULT, ADD)
                 make_d(t, f)
-        third, fourth, fourth_late, fourth_squared = buffer("one"), buffer("two"), buffer("three"), buffer("four")
-        pick_s(2, 0, third)
-        square(third, third)
-        pick_s(3, 0, fourth)
-        square(fourth_squared, fourth)
-        pick_s(3, 1, fourth_late)
-        one_minus(2, 0, buffer("two"), third)
-        one_minus(3, 0, fourth_squared, fourth_squared)
-        late_squared = buffer("one")
-        square(late_squared, fourth_late)
-        one_minus(3, 1, late_squared, late_squared)
+        picked = {(2, 0): buffer("picked20")[:], (2, 1): buffer("picked21")[:], (3, 1): buffer("picked31")[:]}
+        picked[3, 0] = d_first[:, ON_GPSIMD * HALF :].bitcast(F32)
+        for t in range(ON_GPSIMD, PACK):
+            for f in range(2):
+                pick_s(t, f, picked[t, f])
+        square(picked[2, 0], picked[2, 0])
+        one_minus(2, 0, picked[2, 0], picked[2, 0])
+        for t, f in ((3, 0), (2, 1), (3, 1)):
+            squared = buffer("squared")[:]
+            square(squared, picked[t, f])
+            one_minus(t, f, buffer("factor%d%d" % (t, f))[:], squared)
         gain_bank = ps_y.tile([P, HALF], F32, name="acc")
         nc.tensor.transpose(gain_bank[:, 0:P], gain_rows[:], ident[:])
         nc.scalar.copy(out=gain_sb[:], in_=gain_bank[:, 0 : N // P])
         for t in range(ON_GPSIMD, PACK):
             make_d(t, 0)
-        third_late = buffer("two")
-        pick_s(2, 1, third_late)
-        square(third_late, third_late)
-        one_minus(2, 1, third_late, third_late)
         lay_d(0, nc.vector.tensor_copy)
         quantise(d_w[0], d_s[0], d_in[0])
-        make_d(3, 1)
         make_d(2, 1)
+        make_d(3, 1)
         first = [yring.tile([P, S], F32, name="y")]
         make_y(0, 0, first[0])
         place(0, first[0], cols(0), entries(0))

@@ -139,8 +139,8 @@ def tile_list_tied_jet_gradient_kernel(
                         bank[:, P * t : P * (t + 1)], pairs[:, 2 * P * t + u : 2 * P * (t + 1) : 2], ident[:]
                     )
                 nc.scalar.copy(
-                    out=wr_in[a][:].rearrange("m (p u e t) -> m u p e t", u=2, e=2, t=PACK)[:, u],
-                    in_=bank[:].bitcast(BF16).rearrange("m (t p e) -> m p e t", t=PACK, e=2),
+                    out=wr_in[a][:].rearrange("m (p z u e t) -> m u p t z e", z=2, u=2, e=2, t=PACK)[:, u],
+                    in_=bank[:].bitcast(BF16).rearrange("m (t p z e) -> m p t z e", t=PACK, z=2, e=2),
                 )
 
         def pick_s(t, f, target):
@@ -230,6 +230,8 @@ def tile_list_tied_jet_gradient_kernel(
         load_words(c_w[0], c_words[0], slice(0, N))
         load_words(c_w[1], c_words[1], slice(0, N))
         nc.sync.dma_start(out=wgo_sb[:], in_=wgo)
+        pages.append(held("tab_s", [P, T], F32))
+        nc.gpsimd.memset(pages[-1][:], 0.0)
         lay_w(0)
         pick_words(0)
         lay_w(1)
@@ -265,23 +267,22 @@ def tile_list_tied_jet_gradient_kernel(
         quantise(d_w[0], d_s[0], d_in[0])
         make_d(2, 1)
         make_d(3, 1)
-        first = [yring.tile([P, S], F32, name="y")]
-        make_y(0, 0, first[0])
-        place(0, first[0], cols(0), entries(0))
+        first = [yring.tile([P, S], F32, name="y") for b in range(PAGES - 1)]
+        for b in range(PAGES - 1):
+            make_y(b, 0, first[b])
+            place(b, first[b], cols(0), entries(0))
         lay_d(1, nc.scalar.copy)
         quantise(d_w[1], d_s[1], d_in[1])
-        pages.append(held("d_last", [P, T], F32))
-        nc.gpsimd.memset(pages[-1][:], 0.0)
         first.append(held("d_both", [P, S], F32))
-        make_y(1, 0, first[1])
-        place(1, first[1], cols(0), entries(0))
-        for b in range(2):
+        make_y(PAGES - 1, 0, first[-1])
+        place(PAGES - 1, first[-1], cols(0), entries(0))
+        for b in range(PAGES):
             make_y(b, 1, first[b])
             place(b, first[b], cols(1), entries(1))
             store(b)
         turn_w(1)
         quantise(wr_w[1], wr_s[1], wr_in[1][:])
-        for b in range(2, N // P):
+        for b in range(PAGES, N // P):
             y = yring.tile([P, S], F32, name="y")
             for f in range(2):
                 make_y(b, f, y)

@@ -51,7 +51,7 @@ def tile_list_tied_jet_gradient_kernel(
         wk_w = [held("wk_w%d" % a, [P, H], U32) for a in range(2)]
         wk_s = [held("wk_s%d" % a, [P, H], U8) for a in range(2)]
         wr_in = [held("wr_in%d" % a, [P, PACK * PASS], BF16) for a in range(2)]
-        wr_w = [held("wr_w%d" % a, [P, PASS], U32) for a in range(2)]
+        wr_w = [held("wr_w0", [P, PASS], U32)]
         wr_s = [held("wr_s%d" % a, [P, PASS], U8) for a in range(2)]
         s_raw = [held("s_raw%d" % t, [P, T], F32) for t in range(PACK)]
         factor = {(t, f): held("factor%d%d" % (t, f), [P, HALF], F32)[:] for t in range(ON_GPSIMD) for f in range(2)}
@@ -240,12 +240,16 @@ def tile_list_tied_jet_gradient_kernel(
         pick_words(1)
         quantise(wk_w[1], wk_s[1], wk_in[1][:])
         quantise(wr_w[0], wr_s[0], wr_in[0][:])
+        turn_w(1)
         for t in range(ON_GPSIMD):
             for f in range(2):
                 empty_h(t, f)
                 pick_s(t, f, factor[t, f])
                 square(factor[t, f], factor[t, f])
-                nc.gpsimd.tensor_scalar(factor[t, f], factor[t, f], -1.0, 1.0, MULT, ADD)
+                if t == 0:
+                    nc.gpsimd.tensor_scalar(factor[t, f], factor[t, f], -1.0, 1.0, MULT, ADD)
+                else:
+                    one_minus(t, f, factor[t, f], factor[t, f])
                 make_d(t, f)
         picked = {(2, 0): buffer("picked20")[:], (2, 1): buffer("picked21")[:], (3, 1): buffer("picked31")[:]}
         picked[3, 0] = d_first[:, ON_GPSIMD * HALF :].bitcast(F32)
@@ -267,6 +271,8 @@ def tile_list_tied_jet_gradient_kernel(
         quantise(d_w[0], d_s[0], d_in[0])
         make_d(2, 1)
         make_d(3, 1)
+        wr_w.append(held("factor21", [P, PASS], U32))
+        quantise(wr_w[1], wr_s[1], wr_in[1][:])
         first = [yring.tile([P, S], F32, name="y") for b in range(PAGES - 1)]
         for b in range(PAGES - 1):
             make_y(b, 0, first[b])
@@ -280,8 +286,6 @@ def tile_list_tied_jet_gradient_kernel(
             make_y(b, 1, first[b])
             place(b, first[b], cols(1), entries(1))
             store(b)
-        turn_w(1)
-        quantise(wr_w[1], wr_s[1], wr_in[1][:])
         for b in range(PAGES, N // P):
             y = yring.tile([P, S], F32, name="y")
             for f in range(2):

@@ -23,8 +23,10 @@ P = 128
 PACK = 4
 PASS = P * PACK
 HALF = 512
-PAGES = 3
-ON_GPSIMD = 2
+QUARTER = HALF // 2
+PAGES = 4
+COPIED = 2
+LAST = PACK - 1
 
 
 def tile_list_tied_jet_gradient_kernel(
@@ -33,7 +35,7 @@ def tile_list_tied_jet_gradient_kernel(
     nc = tc.nc
     with ExitStack() as ctx:
         keep = ctx.enter_context(tc.tile_pool(name="keep", bufs=1))
-        yring = ctx.enter_context(tc.tile_pool(name="yring", bufs=3))
+        yring = ctx.enter_context(tc.tile_pool(name="yring", bufs=PAGES))
         ps_h = ctx.enter_context(tc.psum_pool(name="ps_h", bufs=4))
         ps_y = ctx.enter_context(tc.psum_pool(name="ps_y", bufs=4))
 
@@ -54,23 +56,24 @@ def tile_list_tied_jet_gradient_kernel(
         wr_w = [held("wr_w0", [P, PASS], U32)]
         wr_s = [held("wr_s%d" % a, [P, PASS], U8) for a in range(2)]
         s_raw = [held("s_raw%d" % t, [P, T], F32) for t in range(PACK)]
-        factor = {(t, f): held("factor%d%d" % (t, f), [P, HALF], F32)[:] for t in range(ON_GPSIMD) for f in range(2)}
-        h_sb = [[held("h_sb%d%d" % (t, f), [P, HALF], F32) for f in range(2)] for t in range(ON_GPSIMD)]
-        d_first = held("d_first", [P, PACK * HALF], BF16)
-        d_both = held("d_both", [P, (PACK + ON_GPSIMD) * HALF], BF16)
-        d_last = held("d_last", [P, PACK * HALF], BF16)
-        d_rows = [d_first[:], d_both[:, 0 : PACK * HALF]]
-        d_in = [d_both[:, ON_GPSIMD * HALF :], d_last[:]]
+        picked = [[held("picked%d%d" % (t, f), [P, HALF], F32) for f in range(2)] for t in range(PACK)]
+        h_sb = [[held("h_sb%d" % t, [P, HALF], F32)[:]] for t in range(PACK)]
+        d_a = held("d_a", [P, PACK * HALF], BF16)
+        d_b = held("d_b", [P, PACK * HALF], BF16)
+        d_c = held("d_c", [P, PACK * HALF], BF16)
+        d_rows = [d_a[:], d_b[:]]
+        d_in = [d_b[:], d_c[:]]
         d_w = [held("d_w%d" % f, [P, HALF], U32) for f in range(2)]
         d_s = [held("d_s%d" % f, [P, HALF], U8) for f in range(2)]
         c_w = [held("c_w%d" % a, [P, N], U32) for a in range(2)]
         c_s = held("c_s", [P, 2, N], U8)
         slope_sb = held("slope_sb", [P, PACK], F32)
+        minus_slope = held("minus_slope", [P, PACK], F32)
         gain_rows = held("gain_rows", [P, P], F32)
         gain_sb = held("gain_sb", [P, N // P], F32)
         wgo_sb = held("wgo_sb", [P, S], F32)
         ident = held("ident", [P, P], F32)
-        pages = [held("page%d" % g, [P, T], F32) for g in range(PAGES - 1)]
+        pages = [held("page%d" % g, [P, T], F32) for g in range(2)]
 
         def cols(f):
             return slice(f * HALF, (f + 1) * HALF)
@@ -143,20 +146,13 @@ def tile_list_tied_jet_gradient_kernel(
                     in_=bank[:].bitcast(BF16).rearrange("m (t p z e) -> m p t z e", t=PACK, z=2, e=2),
                 )
 
-        def pick_s(t, f, target):
-            nc.vector.tensor_copy(target, s_raw[t][:].indirect(idx[:, entries(f)]))
+        def pick_s(t, target, first, count):
+            nc.vector.tensor_copy(target, s_raw[t][:].indirect(idx[:, first // 16 : (first + count) // 16]))
 
         def square(result, values):
             nc.scalar.activation(result, values, SQUARE)
 
-        def one_minus(t, f, result, values):
-            factor[t, f] = result
-            nc.scalar.activation(result, values, COPY, bias=1.0, scale=-1.0)
-
-        def buffer(name):
-            return held(name, [P, HALF], F32)
-
-        def make_h(t, f):
+        def empty_h(t, f):
             h = ps_h.tile([P, HALF], F32, name="h")
             for a in range(2):
                 nc.tensor.matmul_mx(
@@ -168,26 +164,18 @@ def tile_list_tied_jet_gradient_kernel(
                     start=(a == 0),
                     stop=(a == 1),
                 )
-            return h
+            nc.scalar.activation(h_sb[t][f], h[:], COPY, scale=minus_slope[:, t : t + 1])
 
-        def empty_h(t, f):
-            nc.scalar.activation(h_sb[t][f][:], make_h(t, f)[:], COPY, scale=slope_sb[:, t : t + 1])
+        def make_d(t, f, factor):
+            nc.gpsimd.tensor_tensor(d_rows[f][:, cols(t)], h_sb[t][f], factor, MULT)
 
-        def make_d(t, f):
-            if t < ON_GPSIMD:
-                nc.gpsimd.tensor_tensor(d_rows[f][:, cols(t)], h_sb[t][f][:], factor[t, f], MULT)
-            else:
-                nc.vector.scalar_tensor_tensor(
-                    d_rows[f][:, cols(t)], make_h(t, f)[:], slope_sb[:, t : t + 1], factor[t, f], MULT, MULT
-                )
-
-        def lay_d(f, copy):
+        def lay_d(f, copy, runs):
             copy(
-                out=d_in[f].rearrange("p (c i t) -> p c t i", t=PACK, i=4),
-                in_=d_rows[f].rearrange("p (t c i) -> p c t i", t=PACK, i=4),
+                out=d_in[f].rearrange("p (c i t) -> p c t i", t=PACK, i=4)[:, runs],
+                in_=d_rows[f].rearrange("p (t c i) -> p c t i", t=PACK, i=4)[:, runs],
             )
 
-        def make_y(b, f, y):
+        def sum_y(b, f):
             acc = ps_y.tile([P, HALF], F32, name="acc")
             for a in range(2):
                 nc.tensor.matmul_mx(
@@ -209,10 +197,16 @@ def tile_list_tied_jet_gradient_kernel(
                 start=False,
                 stop=True,
             )
-            nc.scalar.activation(y[:, cols(f)], acc[:], COPY, scale=gain_sb[:, b : b + 1])
+            return acc
+
+        def make_y(b, f, y):
+            nc.scalar.activation(y[:, cols(f)], sum_y(b, f)[:], COPY, scale=gain_sb[:, b : b + 1])
 
         def place(b, y, part, ent):
             nc.vector.tensor_tensor(pages[b % PAGES][:].indirect(idx2[:, ent]), y[:, part], wgo_sb[:, part], MULT)
+
+        def place_copy(b, y, part, ent):
+            nc.vector.tensor_copy(pages[b % PAGES][:].indirect(idx2[:, ent]), y[:, part])
 
         def store(b):
             nc.sync.dma_start(out=out[P * b : P * (b + 1), :], in_=pages[b % PAGES][:])
@@ -237,51 +231,64 @@ def tile_list_tied_jet_gradient_kernel(
         lay_w(1)
         turn_w(0)
         quantise(wk_w[0], wk_s[0], wk_in[0][:])
-        pick_words(1)
+        for f in range(2):
+            nc.vector.tensor_copy(v_w[1][:, cols(f)], tab_w[1][:].indirect(idx[:, entries(f)]))
         quantise(wk_w[1], wk_s[1], wk_in[1][:])
         quantise(wr_w[0], wr_s[0], wr_in[0][:])
         turn_w(1)
-        for t in range(ON_GPSIMD):
+        nc.gpsimd.tensor_scalar(minus_slope[:], slope_sb[:], -1.0, 0.0, MULT, ADD)
+        for t in range(LAST):
+            empty_h(t, 0)
             for f in range(2):
-                empty_h(t, f)
-                pick_s(t, f, factor[t, f])
-                square(factor[t, f], factor[t, f])
-                if t == 0:
-                    nc.gpsimd.tensor_scalar(factor[t, f], factor[t, f], -1.0, 1.0, MULT, ADD)
-                else:
-                    one_minus(t, f, factor[t, f], factor[t, f])
-                make_d(t, f)
-        picked = {(2, 0): buffer("picked20")[:], (2, 1): buffer("picked21")[:], (3, 1): buffer("picked31")[:]}
-        picked[3, 0] = d_first[:, ON_GPSIMD * HALF :].bitcast(F32)
-        for t in range(ON_GPSIMD, PACK):
-            for f in range(2):
-                pick_s(t, f, picked[t, f])
-        square(picked[2, 0], picked[2, 0])
-        one_minus(2, 0, picked[2, 0], picked[2, 0])
-        for t, f in ((3, 0), (2, 1), (3, 1)):
-            squared = buffer("squared")[:]
-            square(squared, picked[t, f])
-            one_minus(t, f, buffer("factor%d%d" % (t, f))[:], squared)
+                pick_s(t, picked[t][f][:], f * HALF, HALF)
+            square(picked[t][0][:], picked[t][0][:])
+            nc.gpsimd.tensor_scalar(picked[t][0][:], picked[t][0][:], 1.0, -1.0, MULT, ADD)
+            make_d(t, 0, picked[t][0][:])
+        empty_h(LAST, 0)
         gain_bank = ps_y.tile([P, HALF], F32, name="acc")
         nc.tensor.transpose(gain_bank[:, 0:P], gain_rows[:], ident[:])
         nc.scalar.copy(out=gain_sb[:], in_=gain_bank[:, 0 : N // P])
-        for t in range(ON_GPSIMD, PACK):
-            make_d(t, 0)
-        lay_d(0, nc.vector.tensor_copy)
-        quantise(d_w[0], d_s[0], d_in[0])
-        make_d(2, 1)
-        make_d(3, 1)
-        wr_w.append(held("factor21", [P, PASS], U32))
+        pick_s(LAST, picked[LAST][0][:], 0, HALF)
+        pick_s(LAST, picked[LAST][1][:, 0:QUARTER], HALF, QUARTER)
+        square(picked[LAST][0][:], picked[LAST][0][:])
+        nc.vector.scalar_tensor_tensor(d_rows[0][:, cols(LAST)], picked[LAST][0][:], -1.0, h_sb[LAST][0], ADD, MULT)
+        wr_w.append(held("picked%d0" % LAST, [P, PASS], U32))
         quantise(wr_w[1], wr_s[1], wr_in[1][:])
+        lay_d(0, nc.scalar.copy, slice(0, HALF // 8))
+        lay_d(0, nc.vector.tensor_copy, slice(HALF // 8, HALF // 4))
+        quantise(d_w[0], d_s[0], d_in[0])
+        late = d_rows[1][:, cols(LAST)].bitcast(F32)
+        pick_s(LAST, late, HALF + QUARTER, QUARTER)
         first = [yring.tile([P, S], F32, name="y") for b in range(PAGES - 1)]
-        for b in range(PAGES - 1):
+        nc.vector.scalar_tensor_tensor(first[0][:, cols(0)], sum_y(0, 0)[:], gain_sb[:, 0:1], wgo_sb[:, cols(0)], MULT, MULT)
+        place_copy(0, first[0], cols(0), entries(0))
+        unweighted = held("unweighted", [P, HALF], F32)
+        make_y(1, 0, unweighted)
+        nc.gpsimd.tensor_tensor(first[1][:, cols(0)], unweighted[:], wgo_sb[:, cols(0)], MULT)
+        place_copy(1, first[1], cols(0), entries(0))
+        spent = d_a[:].bitcast(F32)
+        after = held("unweighted", [P, S], F32)
+        second = held("h_sb%d" % LAST, [P, PACK * HALF], F32)
+        for t in range(PACK):
+            h_sb[t].append(second[:, cols(t)])
+        less_one = [spent[:, cols(0)], spent[:, cols(1)], after[:, cols(0)], after[:, cols(1)]]
+        for t in range(PACK):
+            empty_h(t, 1)
+            if t < LAST:
+                square(picked[t][1][:], picked[t][1][:])
+            else:
+                square(picked[t][1][:, 0:QUARTER], picked[t][1][:, 0:QUARTER])
+                square(picked[t][1][:, QUARTER:HALF], late)
+            nc.scalar.activation(less_one[t], picked[t][1][:], COPY, bias=-1.0, scale=1.0)
+            make_d(t, 1, less_one[t])
+        pages.append(held("h_sb%d" % LAST, [P, T], F32))
+        nc.gpsimd.memset(pages[-1][:], 0.0)
+        lay_d(1, nc.scalar.copy, slice(0, HALF // 4))
+        quantise(d_w[1], d_s[1], d_in[1])
+        first.append(held("unweighted", [P, S], F32))
+        for b in range(COPIED, PAGES):
             make_y(b, 0, first[b])
             place(b, first[b], cols(0), entries(0))
-        lay_d(1, nc.scalar.copy)
-        quantise(d_w[1], d_s[1], d_in[1])
-        first.append(held("d_both", [P, S], F32))
-        make_y(PAGES - 1, 0, first[-1])
-        place(PAGES - 1, first[-1], cols(0), entries(0))
         for b in range(PAGES):
             make_y(b, 1, first[b])
             place(b, first[b], cols(1), entries(1))

@@ -25,7 +25,7 @@ PASS = P * PACK
 HALF = 512
 QUARTER = HALF // 2
 PAGES = 4
-COPIED = 2
+COPIED = 3
 LAST = PACK - 1
 
 
@@ -237,6 +237,8 @@ def tile_list_tied_jet_gradient_kernel(
         quantise(wr_w[0], wr_s[0], wr_in[0][:])
         turn_w(1)
         nc.gpsimd.tensor_scalar(minus_slope[:], slope_sb[:], -1.0, 0.0, MULT, ADD)
+        pages.append(held("wk_in1", [P, T], F32))
+        nc.gpsimd.memset(pages[-1][:], 0.0)
         for t in range(LAST):
             empty_h(t, 0)
             for f in range(2):
@@ -266,6 +268,9 @@ def tile_list_tied_jet_gradient_kernel(
         make_y(1, 0, unweighted)
         nc.gpsimd.tensor_tensor(first[1][:, cols(0)], unweighted[:], wgo_sb[:, cols(0)], MULT)
         place_copy(1, first[1], cols(0), entries(0))
+        make_y(2, 0, first[2])
+        nc.gpsimd.tensor_tensor(first[2][:, cols(0)], first[2][:, cols(0)], wgo_sb[:, cols(0)], MULT)
+        place_copy(2, first[2], cols(0), entries(0))
         spent = d_a[:].bitcast(F32)
         after = held("unweighted", [P, S], F32)
         second = held("h_sb%d" % LAST, [P, PACK * HALF], F32)
@@ -281,8 +286,6 @@ def tile_list_tied_jet_gradient_kernel(
                 square(picked[t][1][:, QUARTER:HALF], late)
             nc.scalar.activation(less_one[t], picked[t][1][:], COPY, bias=-1.0, scale=1.0)
             make_d(t, 1, less_one[t])
-        pages.append(held("h_sb%d" % LAST, [P, T], F32))
-        nc.gpsimd.memset(pages[-1][:], 0.0)
         lay_d(1, nc.scalar.copy, slice(0, HALF // 4))
         quantise(d_w[1], d_s[1], d_in[1])
         first.append(held("unweighted", [P, S], F32))

@@ -27,6 +27,7 @@ QUARTER = HALF // 2
 PAGES = 4
 COPIED = 3
 LAST = PACK - 1
+SHARE = 44
 
 
 def tile_list_tied_jet_gradient_kernel(
@@ -52,7 +53,7 @@ def tile_list_tied_jet_gradient_kernel(
         wk_in = [held("wk_in%d" % a, [P, PACK * H], BF16) for a in range(2)]
         wk_w = [held("wk_w%d" % a, [P, H], U32) for a in range(2)]
         wk_s = [held("wk_s%d" % a, [P, H], U8) for a in range(2)]
-        wr_in = [held("wr_in%d" % a, [P, PACK * PASS], BF16) for a in range(2)]
+        wr_in = [held("wr_in0", [P, PACK * PASS], BF16)]
         wr_w = [held("wr_w0", [P, PASS], U32)]
         wr_s = [held("wr_s%d" % a, [P, PASS], U8) for a in range(2)]
         s_raw = [held("s_raw%d" % t, [P, T], F32) for t in range(PACK)]
@@ -235,9 +236,8 @@ def tile_list_tied_jet_gradient_kernel(
             nc.vector.tensor_copy(v_w[1][:, cols(f)], tab_w[1][:].indirect(idx[:, entries(f)]))
         quantise(wk_w[1], wk_s[1], wk_in[1][:])
         quantise(wr_w[0], wr_s[0], wr_in[0][:])
-        turn_w(1)
         nc.gpsimd.tensor_scalar(minus_slope[:], slope_sb[:], -1.0, 0.0, MULT, ADD)
-        pages.append(held("wk_in1", [P, T], F32))
+        pages.append(held("wr_in0", [P, T], F32))
         nc.gpsimd.memset(pages[-1][:], 0.0)
         for t in range(LAST):
             empty_h(t, 0)
@@ -254,10 +254,8 @@ def tile_list_tied_jet_gradient_kernel(
         pick_s(LAST, picked[LAST][1][:, 0:QUARTER], HALF, QUARTER)
         square(picked[LAST][0][:], picked[LAST][0][:])
         nc.vector.scalar_tensor_tensor(d_rows[0][:, cols(LAST)], picked[LAST][0][:], -1.0, h_sb[LAST][0], ADD, MULT)
-        wr_w.append(held("picked%d0" % LAST, [P, PASS], U32))
-        quantise(wr_w[1], wr_s[1], wr_in[1][:])
-        lay_d(0, nc.scalar.copy, slice(0, HALF // 8))
-        lay_d(0, nc.vector.tensor_copy, slice(HALF // 8, HALF // 4))
+        lay_d(0, nc.scalar.copy, slice(0, SHARE))
+        lay_d(0, nc.vector.tensor_copy, slice(SHARE, HALF // 4))
         quantise(d_w[0], d_s[0], d_in[0])
         late = d_rows[1][:, cols(LAST)].bitcast(F32)
         pick_s(LAST, late, HALF + QUARTER, QUARTER)
@@ -292,6 +290,10 @@ def tile_list_tied_jet_gradient_kernel(
         for b in range(COPIED, PAGES):
             make_y(b, 0, first[b])
             place(b, first[b], cols(0), entries(0))
+        wr_in.append(held("d_b", [P, PACK * PASS], BF16))
+        turn_w(1)
+        wr_w.append(held("wr_w1", [P, PASS], U32))
+        quantise(wr_w[1], wr_s[1], wr_in[1][:])
         for b in range(PAGES):
             make_y(b, 1, first[b])
             place(b, first[b], cols(1), entries(1))

@@ -25,7 +25,7 @@ PASS = P * PACK
 HALF = 512
 QUARTER = HALF // 2
 PAGES = 4
-COPIED = 3
+COPIED = 2
 LAST = PACK - 1
 SHARE = 44
 
@@ -58,7 +58,7 @@ def tile_list_tied_jet_gradient_kernel(
         wr_s = [held("wr_s%d" % a, [P, PASS], U8) for a in range(2)]
         s_raw = [held("s_raw%d" % t, [P, T], F32) for t in range(PACK)]
         picked = [[held("picked%d%d" % (t, f), [P, HALF], F32) for f in range(2)] for t in range(PACK)]
-        h_sb = [[held("h_sb%d" % t, [P, HALF], F32)[:]] for t in range(PACK)]
+        h_sb = [[held("h_first", [P, HALF], F32)[:]]] + [[picked[t][0][:]] for t in range(LAST)]
         d_a = held("d_a", [P, PACK * HALF], BF16)
         d_b = held("d_b", [P, PACK * HALF], BF16)
         d_c = held("d_c", [P, PACK * HALF], BF16)
@@ -95,13 +95,14 @@ def tile_list_tied_jet_gradient_kernel(
                 out=tile[:, part].bitcast(I32), in_=words.rearrange("p t i -> p (t i)").bitcast(I32)[:, part]
             )
 
-        def load_w(a):
-            nc.sync.dma_start(out=w_raw[a][:], in_=w[PASS * a : PASS * (a + 1), :].rearrange("(p i) r -> p i r", i=PACK))
+        def load_w(a, part):
+            rows = w[PASS * a : PASS * (a + 1), :].rearrange("(p i) r -> p i r", i=PACK)
+            nc.sync.dma_start(out=w_raw[a][:, part], in_=rows[:, part])
 
         def load_s(t, part):
             nc.sync.dma_start(out=s_raw[t][:, part], in_=sT.rearrange("(p t) x -> p t x", t=PACK)[:, t, part])
 
-        load_w(0)
+        load_w(0, slice(0, PACK))
         nc.sync.dma_start(idx[:], offs)
         for r in range(4):
             nc.sync.dma_start(
@@ -109,14 +110,13 @@ def tile_list_tied_jet_gradient_kernel(
                 in_=tab_scales.bitcast(I32)[:, r:16:4, :].rearrange("a q n -> q a n"),
             )
         load_words(tab_w[0], tab_words[0], slice(0, T))
-        load_w(1)
+        load_w(1, slice(0, 2))
+        load_w(1, slice(2, PACK))
         load_words(tab_w[1], tab_words[1], slice(0, T // 2))
         load_words(tab_w[1], tab_words[1], slice(T // 2, T))
         nc.sync.dma_start(out=slope_sb[:], in_=slope.rearrange("(p t) -> p t", t=PACK))
         nc.sync.dma_start(out=gain_rows[0 : N // P, :], in_=gain.rearrange("(b p) -> b p", p=P))
         nc.sync.dma_start(idx2[:], offs2)
-        load_s(0, slice(0, T // 2))
-        load_s(0, slice(T // 2, T))
 
         def pick_words(a):
             nc.vector.tensor_copy(v_w[a][:], tab_w[a][:].indirect(idx[:]))
@@ -215,7 +215,7 @@ def tile_list_tied_jet_gradient_kernel(
         whole, all_entries = slice(0, S), slice(0, S // 16)
 
         pick_scales()
-        for t in range(1, PACK):
+        for t in range(PACK):
             load_s(t, slice(0, T))
         for q in range(4):
             nc.sync.dma_start(
@@ -243,9 +243,10 @@ def tile_list_tied_jet_gradient_kernel(
             empty_h(t, 0)
             for f in range(2):
                 pick_s(t, picked[t][f][:], f * HALF, HALF)
-            square(picked[t][0][:], picked[t][0][:])
-            nc.gpsimd.tensor_scalar(picked[t][0][:], picked[t][0][:], 1.0, -1.0, MULT, ADD)
-            make_d(t, 0, picked[t][0][:])
+            factor = held("factor%d" % t, [P, HALF], F32)
+            square(factor[:], picked[t][0][:])
+            nc.gpsimd.tensor_scalar(factor[:], factor[:], 1.0, -1.0, MULT, ADD)
+            make_d(t, 0, factor[:])
         empty_h(LAST, 0)
         gain_bank = ps_y.tile([P, HALF], F32, name="acc")
         nc.tensor.transpose(gain_bank[:, 0:P], gain_rows[:], ident[:])
@@ -260,21 +261,19 @@ def tile_list_tied_jet_gradient_kernel(
         late = d_rows[1][:, cols(LAST)].bitcast(F32)
         pick_s(LAST, late, HALF + QUARTER, QUARTER)
         first = [yring.tile([P, S], F32, name="y") for b in range(PAGES - 1)]
-        nc.vector.scalar_tensor_tensor(first[0][:, cols(0)], sum_y(0, 0)[:], gain_sb[:, 0:1], wgo_sb[:, cols(0)], MULT, MULT)
-        place_copy(0, first[0], cols(0), entries(0))
-        unweighted = held("unweighted", [P, HALF], F32)
-        make_y(1, 0, unweighted)
-        nc.gpsimd.tensor_tensor(first[1][:, cols(0)], unweighted[:], wgo_sb[:, cols(0)], MULT)
-        place_copy(1, first[1], cols(0), entries(0))
-        make_y(2, 0, first[2])
-        nc.gpsimd.tensor_tensor(first[2][:, cols(0)], first[2][:, cols(0)], wgo_sb[:, cols(0)], MULT)
-        place_copy(2, first[2], cols(0), entries(0))
+        for b in range(COPIED):
+            nc.vector.scalar_tensor_tensor(
+                first[b][:, cols(0)], sum_y(b, 0)[:], gain_sb[:, b : b + 1], wgo_sb[:, cols(0)], MULT, MULT
+            )
+        for b in range(COPIED):
+            place_copy(b, first[b], cols(0), entries(0))
+        make_y(COPIED, 0, first[COPIED])
+        place(COPIED, first[COPIED], cols(0), entries(0))
         spent = d_a[:].bitcast(F32)
-        after = held("unweighted", [P, S], F32)
-        second = held("h_sb%d" % LAST, [P, PACK * HALF], F32)
+        second = held("picked%d0" % LAST, [P, (PACK + 1) * HALF], F32)
         for t in range(PACK):
             h_sb[t].append(second[:, cols(t)])
-        less_one = [spent[:, cols(0)], spent[:, cols(1)], after[:, cols(0)], after[:, cols(1)]]
+        less_one = [spent[:, cols(0)], spent[:, cols(1)], second[:, cols(PACK)], picked[LAST][1][:]]
         for t in range(PACK):
             empty_h(t, 1)
             if t < LAST:
@@ -286,8 +285,8 @@ def tile_list_tied_jet_gradient_kernel(
             make_d(t, 1, less_one[t])
         lay_d(1, nc.scalar.copy, slice(0, HALF // 4))
         quantise(d_w[1], d_s[1], d_in[1])
-        first.append(held("unweighted", [P, S], F32))
-        for b in range(COPIED, PAGES):
+        first.append(held("picked%d0" % LAST, [P, S], F32))
+        for b in range(PAGES - 1, PAGES):
             make_y(b, 0, first[b])
             place(b, first[b], cols(0), entries(0))
         wr_in.append(held("d_b", [P, PACK * PASS], BF16))

@@ -23,7 +23,6 @@ P = 128
 PACK = 4
 PASS = P * PACK
 HALF = 512
-QUARTER = HALF // 2
 PAGES = 4
 COPIED = 2
 LAST = PACK - 1
@@ -53,7 +52,7 @@ def tile_list_tied_jet_gradient_kernel(
         wk_in = [held("wk_in%d" % a, [P, PACK * H], BF16) for a in range(2)]
         wk_w = [held("wk_w%d" % a, [P, H], U32) for a in range(2)]
         wk_s = [held("wk_s%d" % a, [P, H], U8) for a in range(2)]
-        wr_in = [held("wr_in0", [P, PACK * PASS], BF16)]
+        wr_in = [held("wr_in%d" % a, [P, PACK * PASS], BF16) for a in range(2)]
         wr_w = [held("wr_w0", [P, PASS], U32)]
         wr_s = [held("wr_s%d" % a, [P, PASS], U8) for a in range(2)]
         s_raw = [held("s_raw%d" % t, [P, T], F32) for t in range(PACK)]
@@ -61,9 +60,8 @@ def tile_list_tied_jet_gradient_kernel(
         h_sb = [[held("h_first", [P, HALF], F32)[:]]] + [[picked[t][0][:]] for t in range(LAST)]
         d_a = held("d_a", [P, PACK * HALF], BF16)
         d_b = held("d_b", [P, PACK * HALF], BF16)
-        d_c = held("d_c", [P, PACK * HALF], BF16)
         d_rows = [d_a[:], d_b[:]]
-        d_in = [d_b[:], d_c[:]]
+        d_in = [held("d_in%d" % f, [P, PACK * HALF], BF16)[:] for f in range(2)]
         d_w = [held("d_w%d" % f, [P, HALF], U32) for f in range(2)]
         d_s = [held("d_s%d" % f, [P, HALF], U8) for f in range(2)]
         c_w = [held("c_w%d" % a, [P, N], U32) for a in range(2)]
@@ -217,14 +215,16 @@ def tile_list_tied_jet_gradient_kernel(
         pick_scales()
         for t in range(PACK):
             load_s(t, slice(0, T))
+        nc.sync.dma_start(out=wgo_sb[:, cols(0)], in_=wgo[:, cols(0)])
         for q in range(4):
             nc.sync.dma_start(
                 out=c_s[32 * q : 32 * q + 4, :, :].bitcast(I32),
                 in_=c_scales.bitcast(I32)[:, 4 * q : 4 * q + 4, :].rearrange("a q n -> q a n"),
             )
-        load_words(c_w[0], c_words[0], slice(0, N))
-        load_words(c_w[1], c_words[1], slice(0, N))
-        nc.sync.dma_start(out=wgo_sb[:], in_=wgo)
+        for f in range(2):
+            for a in range(2):
+                load_words(c_w[a], c_words[a], cols(f))
+        nc.sync.dma_start(out=wgo_sb[:, cols(1)], in_=wgo[:, cols(1)])
         pages.append(held("tab_s", [P, T], F32))
         nc.gpsimd.memset(pages[-1][:], 0.0)
         lay_w(0)
@@ -236,6 +236,7 @@ def tile_list_tied_jet_gradient_kernel(
             nc.vector.tensor_copy(v_w[1][:, cols(f)], tab_w[1][:].indirect(idx[:, entries(f)]))
         quantise(wk_w[1], wk_s[1], wk_in[1][:])
         quantise(wr_w[0], wr_s[0], wr_in[0][:])
+        turn_w(1)
         nc.gpsimd.tensor_scalar(minus_slope[:], slope_sb[:], -1.0, 0.0, MULT, ADD)
         pages.append(held("wr_in0", [P, T], F32))
         nc.gpsimd.memset(pages[-1][:], 0.0)
@@ -251,48 +252,41 @@ def tile_list_tied_jet_gradient_kernel(
         gain_bank = ps_y.tile([P, HALF], F32, name="acc")
         nc.tensor.transpose(gain_bank[:, 0:P], gain_rows[:], ident[:])
         nc.scalar.copy(out=gain_sb[:], in_=gain_bank[:, 0 : N // P])
-        pick_s(LAST, picked[LAST][0][:], 0, HALF)
-        pick_s(LAST, picked[LAST][1][:, 0:QUARTER], HALF, QUARTER)
+        for f in range(2):
+            pick_s(LAST, picked[LAST][f][:], f * HALF, HALF)
         square(picked[LAST][0][:], picked[LAST][0][:])
         nc.vector.scalar_tensor_tensor(d_rows[0][:, cols(LAST)], picked[LAST][0][:], -1.0, h_sb[LAST][0], ADD, MULT)
         lay_d(0, nc.scalar.copy, slice(0, SHARE))
         lay_d(0, nc.vector.tensor_copy, slice(SHARE, HALF // 4))
         quantise(d_w[0], d_s[0], d_in[0])
-        late = d_rows[1][:, cols(LAST)].bitcast(F32)
-        pick_s(LAST, late, HALF + QUARTER, QUARTER)
+        wr_w.append(held("d_a", [P, PASS], U32))
+        quantise(wr_w[1], wr_s[1], wr_in[1][:])
         first = [yring.tile([P, S], F32, name="y") for b in range(PAGES - 1)]
+        lent = d_b[:].bitcast(F32)
+        weight = [held("weight0", [P, HALF], F32)[:], lent[:, cols(0)]]
         for b in range(COPIED):
-            nc.vector.scalar_tensor_tensor(
-                first[b][:, cols(0)], sum_y(b, 0)[:], gain_sb[:, b : b + 1], wgo_sb[:, cols(0)], MULT, MULT
-            )
+            nc.scalar.activation(weight[b], wgo_sb[:, cols(0)], COPY, scale=gain_sb[:, b : b + 1])
+        for b in range(COPIED):
+            nc.vector.tensor_tensor(first[b][:, cols(0)], sum_y(b, 0)[:], weight[b], MULT)
         for b in range(COPIED):
             place_copy(b, first[b], cols(0), entries(0))
-        make_y(COPIED, 0, first[COPIED])
-        place(COPIED, first[COPIED], cols(0), entries(0))
-        spent = d_a[:].bitcast(F32)
-        second = held("picked%d0" % LAST, [P, (PACK + 1) * HALF], F32)
+        nc.scalar.activation(lent[:, cols(1)], sum_y(COPIED, 0)[:], COPY, scale=gain_sb[:, COPIED : COPIED + 1])
+        nc.gpsimd.tensor_tensor(first[COPIED][:, cols(0)], lent[:, cols(1)], wgo_sb[:, cols(0)], MULT)
+        place_copy(COPIED, first[COPIED], cols(0), entries(0))
+        second = [held(name, [P, PACK * HALF], F32) for name in ("picked%d0" % LAST, "weight0")]
         for t in range(PACK):
-            h_sb[t].append(second[:, cols(t)])
-        less_one = [spent[:, cols(0)], spent[:, cols(1)], second[:, cols(PACK)], picked[LAST][1][:]]
-        for t in range(PACK):
+            pair, j = divmod(t, 2)
+            h_sb[t].append(second[pair][:, cols(2 * j)])
             empty_h(t, 1)
-            if t < LAST:
-                square(picked[t][1][:], picked[t][1][:])
-            else:
-                square(picked[t][1][:, 0:QUARTER], picked[t][1][:, 0:QUARTER])
-                square(picked[t][1][:, QUARTER:HALF], late)
-            nc.scalar.activation(less_one[t], picked[t][1][:], COPY, bias=-1.0, scale=1.0)
-            make_d(t, 1, less_one[t])
+            square(picked[t][1][:], picked[t][1][:])
+            nc.scalar.activation(second[pair][:, cols(2 * j + 1)], picked[t][1][:], COPY, bias=-1.0, scale=1.0)
+            make_d(t, 1, second[pair][:, cols(2 * j + 1)])
         lay_d(1, nc.scalar.copy, slice(0, HALF // 4))
         quantise(d_w[1], d_s[1], d_in[1])
-        first.append(held("picked%d0" % LAST, [P, S], F32))
+        first.append(held("weight0", [P, S], F32))
         for b in range(PAGES - 1, PAGES):
             make_y(b, 0, first[b])
             place(b, first[b], cols(0), entries(0))
-        wr_in.append(held("d_b", [P, PACK * PASS], BF16))
-        turn_w(1)
-        wr_w.append(held("wr_w1", [P, PASS], U32))
-        quantise(wr_w[1], wr_s[1], wr_in[1][:])
         for b in range(PAGES):
             make_y(b, 1, first[b])
             place(b, first[b], cols(1), entries(1))

@@ -126,11 +126,12 @@ def tile_list_tied_jet_gradient_kernel(
         def quantise(words, scales, values):
             nc.vector.quantize_mx(out=words[:].bitcast(E4M3), scales=scales[:], in_=values)
 
-        def lay_w(a):
-            nc.scalar.copy(
-                out=wk_in[a][:].rearrange("p (t m i) -> p m t i", t=PACK, i=PACK),
-                in_=w_raw[a][:].rearrange("p i (m t) -> p m t i", t=PACK),
-            )
+        def lay_w(a, cut):
+            laid = wk_in[a][:].rearrange("p (t m i) -> p m t i", t=PACK, i=PACK)
+            raw = w_raw[a][:].rearrange("p i (m t) -> p m t i", t=PACK)
+            nc.scalar.copy(out=laid[:, 0:cut], in_=raw[:, 0:cut])
+            if cut < P:
+                nc.gpsimd.tensor_scalar(laid[:, cut:P], raw[:, cut:P], 1.0, 0.0, MULT, ADD)
 
         def turn_w(a):
             pairs = wk_in[a][:].bitcast(F32)
@@ -165,8 +166,8 @@ def tile_list_tied_jet_gradient_kernel(
                 )
             nc.scalar.activation(h_sb[t][f], h[:], COPY, scale=minus_slope[:, t : t + 1])
 
-        def make_d(t, f, factor):
-            nc.gpsimd.tensor_tensor(d_rows[f][:, cols(t)], h_sb[t][f], factor, MULT)
+        def make_d(t, f, factor, part=slice(0, HALF)):
+            nc.gpsimd.tensor_tensor(d_rows[f][:, cols(t)][:, part], h_sb[t][f][:, part], factor[:, part], MULT)
 
         def lay_d(f, copy, runs):
             copy(
@@ -225,12 +226,12 @@ def tile_list_tied_jet_gradient_kernel(
             for a in range(2):
                 load_words(c_w[a], c_words[a], cols(f))
         nc.sync.dma_start(out=wgo_sb[:, cols(1)], in_=wgo[:, cols(1)])
-        pages.append(held("tab_s", [P, T], F32))
+        lay_w(0, P // 2)
+        pages.append(held("w_raw0", [P, T], F32))
         nc.gpsimd.memset(pages[-1][:], 0.0)
-        lay_w(0)
         pick_words(0)
-        lay_w(1)
         turn_w(0)
+        lay_w(1, P)
         quantise(wk_w[0], wk_s[0], wk_in[0][:])
         for f in range(2):
             nc.vector.tensor_copy(v_w[1][:, cols(f)], tab_w[1][:].indirect(idx[:, entries(f)]))
@@ -280,8 +281,12 @@ def tile_list_tied_jet_gradient_kernel(
             empty_h(t, 1)
             square(picked[t][1][:], picked[t][1][:])
             nc.scalar.activation(second[pair][:, cols(2 * j + 1)], picked[t][1][:], COPY, bias=-1.0, scale=1.0)
-            make_d(t, 1, second[pair][:, cols(2 * j + 1)])
-        lay_d(1, nc.scalar.copy, slice(0, HALF // 4))
+            if pair == 0:
+                make_d(t, 1, second[pair][:, cols(2 * j + 1)])
+        for g in range(2):
+            for j in range(2):
+                make_d(2 + j, 1, second[1][:, cols(2 * j + 1)], slice(g * HALF // 2, (g + 1) * HALF // 2))
+            lay_d(1, nc.scalar.copy, slice(g * HALF // 8, (g + 1) * HALF // 8))
         quantise(d_w[1], d_s[1], d_in[1])
         first.append(held("weight0", [P, S], F32))
         for b in range(PAGES - 1, PAGES):

@@ -17,16 +17,16 @@ E5M2 = mybir.dt.float8_e5m2_x4
 MULT = mybir.AluOpType.mult
 ADD = mybir.AluOpType.add
 COPY = mybir.ActivationFunctionType.Copy
+IDENTITY = mybir.ActivationFunctionType.Identity
 SQUARE = mybir.ActivationFunctionType.Square
 
 P = 128
 PACK = 4
 PASS = P * PACK
 HALF = 512
-PAGES = 4
-COPIED = 2
-LAST = PACK - 1
-SHARE = 44
+QUARTER = 256
+PAGES = 3
+PIECES = (slice(0, QUARTER), slice(QUARTER, HALF), slice(HALF, S))
 
 
 def tile_list_tied_jet_gradient_kernel(
@@ -35,12 +35,24 @@ def tile_list_tied_jet_gradient_kernel(
     nc = tc.nc
     with ExitStack() as ctx:
         keep = ctx.enter_context(tc.tile_pool(name="keep", bufs=1))
-        yring = ctx.enter_context(tc.tile_pool(name="yring", bufs=PAGES))
-        ps_h = ctx.enter_context(tc.psum_pool(name="ps_h", bufs=4))
+        yring = ctx.enter_context(tc.tile_pool(name="yring", bufs=PAGES + 1))
+        ps_h = ctx.enter_context(tc.psum_pool(name="ps_h", bufs=1))
         ps_y = ctx.enter_context(tc.psum_pool(name="ps_y", bufs=4))
 
         def held(name, shape, dtype):
             return keep.tile(shape, dtype, name=name, align_bytes=64)
+
+        def width(part):
+            return part.stop - part.start
+
+        def cols(f):
+            return slice(f * HALF, (f + 1) * HALF)
+
+        def quarter(k):
+            return slice(k * QUARTER, (k + 1) * QUARTER)
+
+        def entries(part):
+            return slice(part.start // 16, part.stop // 16)
 
         idx = keep.tile([P, S // 16], U16, name="idx")
         idx2 = keep.tile([P, S // 16], U16, name="idx2")
@@ -56,12 +68,14 @@ def tile_list_tied_jet_gradient_kernel(
         wr_w = [held("wr_w0", [P, PASS], U32)]
         wr_s = [held("wr_s%d" % a, [P, PASS], U8) for a in range(2)]
         s_raw = [held("s_raw%d" % t, [P, T], F32) for t in range(PACK)]
-        picked = [[held("picked%d%d" % (t, f), [P, HALF], F32) for f in range(2)] for t in range(PACK)]
-        h_sb = [[held("h_first", [P, HALF], F32)[:]]] + [[picked[t][0][:]] for t in range(LAST)]
-        d_a = held("d_a", [P, PACK * HALF], BF16)
-        d_b = held("d_b", [P, PACK * HALF], BF16)
-        d_rows = [d_a[:], d_b[:]]
-        d_in = [held("d_in%d" % f, [P, PACK * HALF], BF16)[:] for f in range(2)]
+        picked = [[held("picked%d%d" % (t, f), [P, HALF], F32) for f in range(2)] for t in range(2)]
+        early = [None, [held("early10", [P, HALF], F32)[:], picked[1][1][:]]]
+        late = [[held("late0%d" % k, [P, QUARTER], F32) for k in range(4)]]
+        late.append([held("late1%d" % k, [P, QUARTER], F32) for k in range(3)])
+        h_sb = [[held("h_sb%d" % t, [P, HALF], F32)[:]] for t in range(2)]
+        factor = [held("factor%d" % k, [P, 2 * QUARTER], F32) for k in range(2)]
+        d_in = [held("d_in%d" % j, [P, PACK * width(part)], BF16) for j, part in enumerate(PIECES)]
+        d_pairs = [d_in[0]] + [held("d_pairs%d" % j, [P, PACK * width(PIECES[j])], BF16) for j in range(1, 3)]
         d_w = [held("d_w%d" % f, [P, HALF], U32) for f in range(2)]
         d_s = [held("d_s%d" % f, [P, HALF], U8) for f in range(2)]
         c_w = [held("c_w%d" % a, [P, N], U32) for a in range(2)]
@@ -72,21 +86,17 @@ def tile_list_tied_jet_gradient_kernel(
         gain_sb = held("gain_sb", [P, N // P], F32)
         wgo_sb = held("wgo_sb", [P, S], F32)
         ident = held("ident", [P, P], F32)
-        pages = [held("page%d" % g, [P, T], F32) for g in range(2)]
-
-        def cols(f):
-            return slice(f * HALF, (f + 1) * HALF)
-
-        def entries(f):
-            return slice(f * HALF // 16, (f + 1) * HALF // 16)
+        pages = [held("page%d" % g, [P, T], F32) for g in range(PAGES)]
+        h_late = [ps_h.tile([P, 2 * QUARTER], F32, name="h_late%d" % k) for k in range(4)]
 
         nc.gpsimd.memset(tab_s[:].bitcast(I32), 0)
         nc.gpsimd.memset(gain_rows[:], 0.0)
         nc.gpsimd.memset(v_s[1][:].bitcast(I32), 0)
         make_identity(nc, ident[:])
         nc.gpsimd.memset(c_s[:].bitcast(I32), 0)
-        for page in pages:
+        for page in pages[:-1]:
             nc.vector.memset(page[:], 0.0)
+        nc.gpsimd.memset(pages[-1][:], 0.0)
 
         def load_words(tile, words, part):
             nc.sync.dma_start(
@@ -97,34 +107,34 @@ def tile_list_tied_jet_gradient_kernel(
             rows = w[PASS * a : PASS * (a + 1), :].rearrange("(p i) r -> p i r", i=PACK)
             nc.sync.dma_start(out=w_raw[a][:, part], in_=rows[:, part])
 
-        def load_s(t, part):
-            nc.sync.dma_start(out=s_raw[t][:, part], in_=sT.rearrange("(p t) x -> p t x", t=PACK)[:, t, part])
+        def load_s(t):
+            nc.sync.dma_start(out=s_raw[t][:], in_=sT.rearrange("(p t) x -> p t x", t=PACK)[:, t, :])
 
-        load_w(0, slice(0, PACK))
+        load_words(tab_w[0], tab_words[0], slice(0, T))
         nc.sync.dma_start(idx[:], offs)
         for r in range(4):
             nc.sync.dma_start(
                 out=tab_s[r:P:16, :].bitcast(I32),
                 in_=tab_scales.bitcast(I32)[:, r:16:4, :].rearrange("a q n -> q a n"),
             )
-        load_words(tab_w[0], tab_words[0], slice(0, T))
-        load_w(1, slice(0, 2))
-        load_w(1, slice(2, PACK))
+        load_w(0, slice(0, PACK))
+        load_s(0)
+        load_w(1, slice(0, PACK))
         load_words(tab_w[1], tab_words[1], slice(0, T // 2))
         load_words(tab_w[1], tab_words[1], slice(T // 2, T))
         nc.sync.dma_start(out=slope_sb[:], in_=slope.rearrange("(p t) -> p t", t=PACK))
         nc.sync.dma_start(out=gain_rows[0 : N // P, :], in_=gain.rearrange("(b p) -> b p", p=P))
         nc.sync.dma_start(idx2[:], offs2)
 
-        def pick_words(a):
-            nc.vector.tensor_copy(v_w[a][:], tab_w[a][:].indirect(idx[:]))
+        def pick_words(a, part):
+            nc.vector.tensor_copy(v_w[a][:, part], tab_w[a][:].indirect(idx[:, entries(part)]))
 
         def pick_scales():
             nc.vector.tensor_copy(v_s[0][:], tab_s[:].indirect(idx[:]))
             nc.sync.dma_start(out=v_s[1][0:112, :].bitcast(I32), in_=v_s[0][16:128, :].bitcast(I32))
 
         def quantise(words, scales, values):
-            nc.vector.quantize_mx(out=words[:].bitcast(E4M3), scales=scales[:], in_=values)
+            nc.vector.quantize_mx(out=words.bitcast(E4M3), scales=scales, in_=values)
 
         def lay_w(a, cut):
             laid = wk_in[a][:].rearrange("p (t m i) -> p m t i", t=PACK, i=PACK)
@@ -146,77 +156,119 @@ def tile_list_tied_jet_gradient_kernel(
                     in_=bank[:].bitcast(BF16).rearrange("m (t p z e) -> m p t z e", t=PACK, z=2, e=2),
                 )
 
-        def pick_s(t, target, first, count):
-            nc.vector.tensor_copy(target, s_raw[t][:].indirect(idx[:, first // 16 : (first + count) // 16]))
+        def pick_s(t, target, part):
+            nc.vector.tensor_copy(target, s_raw[t][:].indirect(idx[:, entries(part)]))
 
-        def square(result, values):
-            nc.scalar.activation(result, values, SQUARE)
-
-        def empty_h(t, f):
-            h = ps_h.tile([P, HALF], F32, name="h")
+        def sum_h(bank, t, part):
             for a in range(2):
                 nc.tensor.matmul_mx(
-                    out=h[:],
+                    out=bank,
                     lhsT=wk_w[a][:, P * t : P * (t + 1)].bitcast(E4M3),
                     lhsT_scale=wk_s[a][:, P * t : P * (t + 1)],
-                    rhs=v_w[a][:, cols(f)].bitcast(E5M2),
-                    rhs_scale=v_s[a][:, cols(f)],
+                    rhs=v_w[a][:, part].bitcast(E5M2),
+                    rhs_scale=v_s[a][:, part],
                     start=(a == 0),
                     stop=(a == 1),
                 )
+
+        def empty_h(t, f):
+            h = ps_y.tile([P, HALF], F32, name="acc")
+            sum_h(h[:], t, cols(f))
             nc.scalar.activation(h_sb[t][f], h[:], COPY, scale=minus_slope[:, t : t + 1])
 
-        def make_d(t, f, factor, part=slice(0, HALF)):
-            nc.gpsimd.tensor_tensor(d_rows[f][:, cols(t)][:, part], h_sb[t][f][:, part], factor[:, part], MULT)
+        def early_d(t, j):
+            part = PIECES[j]
+            f = part.start // HALF
+            inside = slice(part.start - f * HALF, part.stop - f * HALF)
+            if j == 0:
+                pairs = d_in[0][:].rearrange("p (c e) -> p c e", e=PACK)
+            else:
+                pairs = d_pairs[j][:, 0 : 2 * width(part)].rearrange("p (c e) -> p c e", e=2)
+            nc.gpsimd.tensor_tensor(pairs[:, :, t], h_sb[t][f][:, inside], early[t][f][:, inside], MULT)
 
-        def lay_d(f, copy, runs):
-            copy(
-                out=d_in[f].rearrange("p (c i t) -> p c t i", t=PACK, i=4)[:, runs],
-                in_=d_rows[f].rearrange("p (t c i) -> p c t i", t=PACK, i=4)[:, runs],
+        def late_square(u, k):
+            values = late[u][k]
+            if (u, k) == (1, 0):
+                late[u][k] = held("early10", [P, QUARTER], F32)
+            nc.scalar.activation(late[u][k][:], values[:], SQUARE)
+
+        def late_factor(u, k):
+            nc.scalar.activation(
+                factor[k][:, quarter(u)],
+                late[u][k][:],
+                IDENTITY,
+                scale=minus_slope[:, 2 + u : 3 + u],
+                bias=slope_sb[:, 2 + u : 3 + u],
             )
 
-        def sum_y(b, f):
+        def late_d(k):
+            if k == 0:
+                pairs = d_in[0][:].rearrange("p (c e) -> p c e", e=PACK)[:, :, 2:PACK]
+            else:
+                j = min(k, 2)
+                first = 2 * width(PIECES[j]) + 2 * QUARTER * (k - j)
+                pairs = d_pairs[j][:, first : first + 2 * QUARTER].rearrange("p (c u) -> p c u", u=2)
+            nc.vector.tensor_tensor(
+                pairs,
+                h_late[k][:].rearrange("p (u c) -> p c u", u=2),
+                factor[k][:].rearrange("p (u c) -> p c u", u=2),
+                MULT,
+            )
+
+        def lay_d(j):
+            nc.scalar.copy(
+                out=d_in[j][:].bitcast(F32).rearrange("p (c u) -> p c u", u=2),
+                in_=d_pairs[j][:].bitcast(F32).rearrange("p (u c) -> p c u", u=2),
+            )
+
+        def quantise_d(j):
+            part = PIECES[j]
+            f = part.start // HALF
+            inside = slice(part.start - f * HALF, part.stop - f * HALF)
+            quantise(d_w[f][:, inside], d_s[f][:, inside], d_in[j][:])
+
+        def make_y(b, part, y):
+            f = part.start // HALF
+            inside = slice(part.start - f * HALF, part.stop - f * HALF)
             acc = ps_y.tile([P, HALF], F32, name="acc")
             for a in range(2):
                 nc.tensor.matmul_mx(
-                    out=acc[:],
+                    out=acc[:, 0 : width(part)],
                     lhsT=c_w[a][:, P * b : P * (b + 1)].bitcast(E4M3),
                     lhsT_scale=c_s[:, a, P * b : P * (b + 1)],
-                    rhs=v_w[a][:, cols(f)].bitcast(E5M2),
-                    rhs_scale=v_s[a][:, cols(f)],
+                    rhs=v_w[a][:, part].bitcast(E5M2),
+                    rhs_scale=v_s[a][:, part],
                     start=(a == 0),
                     stop=False,
                 )
             a, j = divmod(b, PACK)
             nc.tensor.matmul_mx(
-                out=acc[:],
+                out=acc[:, 0 : width(part)],
                 lhsT=wr_w[a][:, P * j : P * (j + 1)].bitcast(E4M3),
                 lhsT_scale=wr_s[a][:, P * j : P * (j + 1)],
-                rhs=d_w[f][:].bitcast(E4M3),
-                rhs_scale=d_s[f][:],
+                rhs=d_w[f][:, inside].bitcast(E4M3),
+                rhs_scale=d_s[f][:, inside],
                 start=False,
                 stop=True,
             )
-            return acc
+            nc.scalar.activation(y, acc[:, 0 : width(part)], COPY, scale=gain_sb[:, b : b + 1])
 
-        def make_y(b, f, y):
-            nc.scalar.activation(y[:, cols(f)], sum_y(b, f)[:], COPY, scale=gain_sb[:, b : b + 1])
-
-        def place(b, y, part, ent):
-            nc.vector.tensor_tensor(pages[b % PAGES][:].indirect(idx2[:, ent]), y[:, part], wgo_sb[:, part], MULT)
-
-        def place_copy(b, y, part, ent):
-            nc.vector.tensor_copy(pages[b % PAGES][:].indirect(idx2[:, ent]), y[:, part])
+        def place(b, y, part):
+            nc.vector.tensor_tensor(
+                pages[b % PAGES][:].indirect(idx2[:, entries(part)]), y, wgo_sb[:, part], MULT
+            )
 
         def store(b):
             nc.sync.dma_start(out=out[P * b : P * (b + 1), :], in_=pages[b % PAGES][:])
 
-        whole, all_entries = slice(0, S), slice(0, S // 16)
+        def early_factor(t, f):
+            nc.scalar.activation(early[t][f], picked[t][f][:], SQUARE)
+            nc.gpsimd.tensor_scalar(early[t][f], early[t][f], 1.0, -1.0, MULT, ADD)
 
+        pick_words(0, slice(0, S))
         pick_scales()
-        for t in range(PACK):
-            load_s(t, slice(0, T))
-        nc.sync.dma_start(out=wgo_sb[:, cols(0)], in_=wgo[:, cols(0)])
+        for t in range(1, PACK):
+            load_s(t)
         for q in range(4):
             nc.sync.dma_start(
                 out=c_s[32 * q : 32 * q + 4, :, :].bitcast(I32),
@@ -225,80 +277,92 @@ def tile_list_tied_jet_gradient_kernel(
         for f in range(2):
             for a in range(2):
                 load_words(c_w[a], c_words[a], cols(f))
-        nc.sync.dma_start(out=wgo_sb[:, cols(1)], in_=wgo[:, cols(1)])
+            nc.sync.dma_start(out=wgo_sb[:, cols(f)], in_=wgo[:, cols(f)])
         lay_w(0, P // 2)
-        pages.append(held("w_raw0", [P, T], F32))
-        nc.gpsimd.memset(pages[-1][:], 0.0)
-        pick_words(0)
+        quantise(wk_w[0][:], wk_s[0][:], wk_in[0][:])
         turn_w(0)
-        lay_w(1, P)
-        quantise(wk_w[0], wk_s[0], wk_in[0][:])
         for f in range(2):
-            nc.vector.tensor_copy(v_w[1][:, cols(f)], tab_w[1][:].indirect(idx[:, entries(f)]))
-        quantise(wk_w[1], wk_s[1], wk_in[1][:])
-        quantise(wr_w[0], wr_s[0], wr_in[0][:])
+            pick_s(0, picked[0][f][:], cols(f))
+        lay_w(1, 5 * P // 8)
+        quantise(wr_w[0][:], wr_s[0][:], wr_in[0][:])
+        quantise(wk_w[1][:], wk_s[1][:], wk_in[1][:])
+        squares = held("w_raw1", [P, S], F32)
+        early[0] = [squares[:, cols(f)] for f in range(2)]
+        for f in range(2):
+            early_factor(0, f)
         turn_w(1)
-        nc.gpsimd.tensor_scalar(minus_slope[:], slope_sb[:], -1.0, 0.0, MULT, ADD)
-        pages.append(held("wr_in0", [P, T], F32))
-        nc.gpsimd.memset(pages[-1][:], 0.0)
-        for t in range(LAST):
+        for f in range(2):
+            pick_words(1, cols(f))
+        nc.scalar.activation(minus_slope[:], slope_sb[:], COPY, scale=-1.0)
+        for t in range(2):
             empty_h(t, 0)
-            for f in range(2):
-                pick_s(t, picked[t][f][:], f * HALF, HALF)
-            factor = held("factor%d" % t, [P, HALF], F32)
-            square(factor[:], picked[t][0][:])
-            nc.gpsimd.tensor_scalar(factor[:], factor[:], 1.0, -1.0, MULT, ADD)
-            make_d(t, 0, factor[:])
-        empty_h(LAST, 0)
+        for f in range(2):
+            pick_s(1, picked[1][f][:], cols(f))
+        early_factor(1, 0)
+        for t in range(2):
+            for j in range(2):
+                early_d(t, j)
+        h_second = held("picked10", [P, S], F32)
+        for t in range(2):
+            h_sb[t].append(h_second[:, cols(t)])
+            empty_h(t, 1)
+        early_d(0, 2)
+        early_factor(1, 1)
+        early_d(1, 2)
+        for k in range(4):
+            for u in range(2):
+                sum_h(h_late[k][:, quarter(u)], 2 + u, quarter(k))
         gain_bank = ps_y.tile([P, HALF], F32, name="acc")
         nc.tensor.transpose(gain_bank[:, 0:P], gain_rows[:], ident[:])
         nc.scalar.copy(out=gain_sb[:], in_=gain_bank[:, 0 : N // P])
-        for f in range(2):
-            pick_s(LAST, picked[LAST][f][:], f * HALF, HALF)
-        square(picked[LAST][0][:], picked[LAST][0][:])
-        nc.vector.scalar_tensor_tensor(d_rows[0][:, cols(LAST)], picked[LAST][0][:], -1.0, h_sb[LAST][0], ADD, MULT)
-        lay_d(0, nc.scalar.copy, slice(0, SHARE))
-        lay_d(0, nc.vector.tensor_copy, slice(SHARE, HALF // 4))
-        quantise(d_w[0], d_s[0], d_in[0])
-        wr_w.append(held("d_a", [P, PASS], U32))
-        quantise(wr_w[1], wr_s[1], wr_in[1][:])
-        first = [yring.tile([P, S], F32, name="y") for b in range(PAGES - 1)]
-        lent = d_b[:].bitcast(F32)
-        weight = [held("weight0", [P, HALF], F32)[:], lent[:, cols(0)]]
-        for b in range(COPIED):
-            nc.scalar.activation(weight[b], wgo_sb[:, cols(0)], COPY, scale=gain_sb[:, b : b + 1])
-        for b in range(COPIED):
-            nc.vector.tensor_tensor(first[b][:, cols(0)], sum_y(b, 0)[:], weight[b], MULT)
-        for b in range(COPIED):
-            place_copy(b, first[b], cols(0), entries(0))
-        nc.scalar.activation(lent[:, cols(1)], sum_y(COPIED, 0)[:], COPY, scale=gain_sb[:, COPIED : COPIED + 1])
-        nc.gpsimd.tensor_tensor(first[COPIED][:, cols(0)], lent[:, cols(1)], wgo_sb[:, cols(0)], MULT)
-        place_copy(COPIED, first[COPIED], cols(0), entries(0))
-        second = [held(name, [P, PACK * HALF], F32) for name in ("picked%d0" % LAST, "weight0")]
-        for t in range(PACK):
-            pair, j = divmod(t, 2)
-            h_sb[t].append(second[pair][:, cols(2 * j)])
-            empty_h(t, 1)
-            square(picked[t][1][:], picked[t][1][:])
-            nc.scalar.activation(second[pair][:, cols(2 * j + 1)], picked[t][1][:], COPY, bias=-1.0, scale=1.0)
-            if pair == 0:
-                make_d(t, 1, second[pair][:, cols(2 * j + 1)])
-        for g in range(2):
-            for j in range(2):
-                make_d(2 + j, 1, second[1][:, cols(2 * j + 1)], slice(g * HALF // 2, (g + 1) * HALF // 2))
-            lay_d(1, nc.scalar.copy, slice(g * HALF // 8, (g + 1) * HALF // 8))
-        quantise(d_w[1], d_s[1], d_in[1])
-        first.append(held("weight0", [P, S], F32))
-        for b in range(PAGES - 1, PAGES):
-            make_y(b, 0, first[b])
-            place(b, first[b], cols(0), entries(0))
+        for k in range(4):
+            pick_s(2, late[0][k][:], quarter(k))
+        for k in range(3):
+            pick_s(3, late[1][k][:], quarter(k))
+        for k in range(4):
+            late_square(0, k)
+            if k < 2:
+                late_factor(0, k)
+        late_square(1, 0)
+        late_factor(1, 0)
+        late_d(0)
+        late[1].append(held("factor0", [P, QUARTER], F32))
+        pick_s(3, late[1][3][:], quarter(3))
+        quantise_d(0)
+        late_square(1, 1)
+        late_factor(1, 1)
+        late_d(1)
+        for k in range(2, 4):
+            factor.append(held(("early10", "late11")[k - 2], [P, 2 * QUARTER], F32))
+            late_factor(0, k)
+        wr_w.append(held("d_in0", [P, PASS], U32))
+        quantise(wr_w[1][:], wr_s[1][:], wr_in[1][:])
+
+        def first_piece(b, name):
+            y = held(name, [P, QUARTER], F32)
+            make_y(b, PIECES[0], y[:])
+            place(b, y[:], PIECES[0])
+
+        first_piece(0, "y_first")
+        for k in range(2, 4):
+            late_square(1, k)
+            late_factor(1, k)
+            late_d(k)
+        lay_d(1)
+        quantise_d(1)
+        first_piece(1, "early10")
+        lay_d(2)
+        quantise_d(2)
+        first_piece(2, "d_pairs2")
         for b in range(PAGES):
-            make_y(b, 1, first[b])
-            place(b, first[b], cols(1), entries(1))
+            y = yring.tile([P, S], F32, name="y")
+            for part in PIECES[1:]:
+                make_y(b, part, y[:, part])
+            place(b, y[:, QUARTER:S], slice(QUARTER, S))
             store(b)
         for b in range(PAGES, N // P):
             y = yring.tile([P, S], F32, name="y")
             for f in range(2):
-                make_y(b, f, y)
-            place(b, y, whole, all_entries)
+                make_y(b, cols(f), y[:, cols(f)])
+            place(b, y[:], slice(0, S))
             store(b)

@@ -68,10 +68,14 @@ def tile_list_tied_jet_gradient_kernel(
         wr_w = [held("wr_w0", [P, PASS], U32)]
         wr_s = [held("wr_s%d" % a, [P, PASS], U8) for a in range(2)]
         s_raw = [held("s_raw%d" % t, [P, T], F32) for t in range(PACK)]
-        picked = [[held("picked%d%d" % (t, f), [P, HALF], F32) for f in range(2)] for t in range(2)]
-        early = [None, [held("early10", [P, HALF], F32)[:], picked[1][1][:]]]
-        late = [[held("late0%d" % k, [P, QUARTER], F32) for k in range(4)]]
-        late.append([held("late1%d" % k, [P, QUARTER], F32) for k in range(3)])
+        picked_first = held("picked_first", [P, S], F32)
+        picked = [[picked_first[:, cols(f)] for f in range(2)]]
+        picked.append([held("picked1%d" % f, [P, HALF], F32)[:] for f in range(2)])
+        early = [None, [held("early10", [P, HALF], F32)[:], picked[1][1]]]
+        third = [held("third%d" % f, [P, HALF], F32) for f in range(2)]
+        fourth = [held("fourth%d" % j, [P, width(part)], F32) for j, part in enumerate(PIECES)]
+        late = [[third[k // 2][:, quarter(k % 2)] for k in range(4)]]
+        late.append([fourth[min(k, 2)][:, quarter(k - min(k, 2))] for k in range(4)])
         h_sb = [[held("h_sb%d" % t, [P, HALF], F32)[:]] for t in range(2)]
         factor = [held("factor%d" % k, [P, 2 * QUARTER], F32) for k in range(2)]
         d_in = [held("d_in%d" % j, [P, PACK * width(part)], BF16) for j, part in enumerate(PIECES)]
@@ -107,8 +111,8 @@ def tile_list_tied_jet_gradient_kernel(
             rows = w[PASS * a : PASS * (a + 1), :].rearrange("(p i) r -> p i r", i=PACK)
             nc.sync.dma_start(out=w_raw[a][:, part], in_=rows[:, part])
 
-        def load_s(t):
-            nc.sync.dma_start(out=s_raw[t][:], in_=sT.rearrange("(p t) x -> p t x", t=PACK)[:, t, :])
+        def load_s(t, part):
+            nc.sync.dma_start(out=s_raw[t][:, part], in_=sT.rearrange("(p t) x -> p t x", t=PACK)[:, t, part])
 
         load_words(tab_w[0], tab_words[0], slice(0, T))
         nc.sync.dma_start(idx[:], offs)
@@ -118,13 +122,13 @@ def tile_list_tied_jet_gradient_kernel(
                 in_=tab_scales.bitcast(I32)[:, r:16:4, :].rearrange("a q n -> q a n"),
             )
         load_w(0, slice(0, PACK))
-        load_s(0)
-        load_w(1, slice(0, PACK))
+        load_s(0, slice(0, T // 2))
+        load_s(0, slice(T // 2, T))
+        load_w(1, slice(0, 2))
+        load_w(1, slice(2, PACK))
         load_words(tab_w[1], tab_words[1], slice(0, T // 2))
         load_words(tab_w[1], tab_words[1], slice(T // 2, T))
         nc.sync.dma_start(out=slope_sb[:], in_=slope.rearrange("(p t) -> p t", t=PACK))
-        nc.sync.dma_start(out=gain_rows[0 : N // P, :], in_=gain.rearrange("(b p) -> b p", p=P))
-        nc.sync.dma_start(idx2[:], offs2)
 
         def pick_words(a, part):
             nc.vector.tensor_copy(v_w[a][:, part], tab_w[a][:].indirect(idx[:, entries(part)]))
@@ -186,16 +190,16 @@ def tile_list_tied_jet_gradient_kernel(
                 pairs = d_pairs[j][:, 0 : 2 * width(part)].rearrange("p (c e) -> p c e", e=2)
             nc.gpsimd.tensor_tensor(pairs[:, :, t], h_sb[t][f][:, inside], early[t][f][:, inside], MULT)
 
-        def late_square(u, k):
-            values = late[u][k]
-            if (u, k) == (1, 0):
-                late[u][k] = held("early10", [P, QUARTER], F32)
-            nc.scalar.activation(late[u][k][:], values[:], SQUARE)
+        def late_square(k):
+            values = late[1][k]
+            if k == 0:
+                late[1][k] = held("early10", [P, QUARTER], F32)[:]
+            nc.scalar.activation(late[1][k], values, SQUARE)
 
         def late_factor(u, k):
             nc.scalar.activation(
                 factor[k][:, quarter(u)],
-                late[u][k][:],
+                late[u][k],
                 IDENTITY,
                 scale=minus_slope[:, 2 + u : 3 + u],
                 bias=slope_sb[:, 2 + u : 3 + u],
@@ -262,13 +266,14 @@ def tile_list_tied_jet_gradient_kernel(
             nc.sync.dma_start(out=out[P * b : P * (b + 1), :], in_=pages[b % PAGES][:])
 
         def early_factor(t, f):
-            nc.scalar.activation(early[t][f], picked[t][f][:], SQUARE)
+            nc.scalar.activation(early[t][f], picked[t][f], SQUARE)
             nc.gpsimd.tensor_scalar(early[t][f], early[t][f], 1.0, -1.0, MULT, ADD)
 
         pick_words(0, slice(0, S))
         pick_scales()
         for t in range(1, PACK):
-            load_s(t)
+            load_s(t, slice(0, T))
+        nc.sync.dma_start(out=gain_rows[0 : N // P, :], in_=gain.rearrange("(b p) -> b p", p=P))
         for q in range(4):
             nc.sync.dma_start(
                 out=c_s[32 * q : 32 * q + 4, :, :].bitcast(I32),
@@ -277,12 +282,13 @@ def tile_list_tied_jet_gradient_kernel(
         for f in range(2):
             for a in range(2):
                 load_words(c_w[a], c_words[a], cols(f))
+            if f == 0:
+                nc.sync.dma_start(idx2[:], offs2)
             nc.sync.dma_start(out=wgo_sb[:, cols(f)], in_=wgo[:, cols(f)])
         lay_w(0, P // 2)
         quantise(wk_w[0][:], wk_s[0][:], wk_in[0][:])
         turn_w(0)
-        for f in range(2):
-            pick_s(0, picked[0][f][:], cols(f))
+        pick_s(0, picked_first[:], slice(0, S))
         lay_w(1, 5 * P // 8)
         quantise(wr_w[0][:], wr_s[0][:], wr_in[0][:])
         quantise(wk_w[1][:], wk_s[1][:], wk_in[1][:])
@@ -297,7 +303,7 @@ def tile_list_tied_jet_gradient_kernel(
         for t in range(2):
             empty_h(t, 0)
         for f in range(2):
-            pick_s(1, picked[1][f][:], cols(f))
+            pick_s(1, picked[1][f], cols(f))
         early_factor(1, 0)
         for t in range(2):
             for j in range(2):
@@ -315,25 +321,23 @@ def tile_list_tied_jet_gradient_kernel(
         gain_bank = ps_y.tile([P, HALF], F32, name="acc")
         nc.tensor.transpose(gain_bank[:, 0:P], gain_rows[:], ident[:])
         nc.scalar.copy(out=gain_sb[:], in_=gain_bank[:, 0 : N // P])
-        for k in range(4):
-            pick_s(2, late[0][k][:], quarter(k))
-        for k in range(3):
-            pick_s(3, late[1][k][:], quarter(k))
-        for k in range(4):
-            late_square(0, k)
-            if k < 2:
-                late_factor(0, k)
-        late_square(1, 0)
+        for f in range(2):
+            pick_s(2, third[f][:], cols(f))
+        for j, part in enumerate(PIECES):
+            pick_s(3, fourth[j][:], part)
+        nc.scalar.activation(third[0][:], third[0][:], SQUARE)
+        for k in range(2):
+            late_factor(0, k)
+        nc.scalar.activation(third[1][:], third[1][:], SQUARE)
+        late_square(0)
         late_factor(1, 0)
         late_d(0)
-        late[1].append(held("factor0", [P, QUARTER], F32))
-        pick_s(3, late[1][3][:], quarter(3))
-        quantise_d(0)
-        late_square(1, 1)
+        late_square(1)
         late_factor(1, 1)
         late_d(1)
+        quantise_d(0)
         for k in range(2, 4):
-            factor.append(held(("early10", "late11")[k - 2], [P, 2 * QUARTER], F32))
+            factor.append(held(("early10", "fourth1")[k - 2], [P, 2 * QUARTER], F32))
             late_factor(0, k)
         wr_w.append(held("d_in0", [P, PASS], U32))
         quantise(wr_w[1][:], wr_s[1][:], wr_in[1][:])
@@ -345,7 +349,7 @@ def tile_list_tied_jet_gradient_kernel(
 
         first_piece(0, "y_first")
         for k in range(2, 4):
-            late_square(1, k)
+            late_square(k)
             late_factor(1, k)
             late_d(k)
         lay_d(1)

@@ -207,15 +207,15 @@ def tile_list_tied_jet_gradient_kernel(
 
         def late_d(k):
             if k == 0:
-                pairs = d_in[0][:].rearrange("p (c e) -> p c e", e=PACK)[:, :, 2:PACK]
+                pairs = d_in[0][:].rearrange("p (c i e) -> p c e i", i=4, e=PACK)[:, :, 2:PACK, :]
             else:
                 j = min(k, 2)
                 first = 2 * width(PIECES[j]) + 2 * QUARTER * (k - j)
-                pairs = d_pairs[j][:, first : first + 2 * QUARTER].rearrange("p (c u) -> p c u", u=2)
+                pairs = d_pairs[j][:, first : first + 2 * QUARTER].rearrange("p (c i u) -> p c u i", i=4, u=2)
             nc.vector.tensor_tensor(
                 pairs,
-                h_late[k][:].rearrange("p (u c) -> p c u", u=2),
-                factor[k][:].rearrange("p (u c) -> p c u", u=2),
+                h_late[k][:].rearrange("p (u c i) -> p c u i", u=2, i=4),
+                factor[k][:].rearrange("p (u c i) -> p c u i", u=2, i=4),
                 MULT,
             )
 

@@ -140,12 +140,11 @@ def tile_list_tied_jet_gradient_kernel(
         def quantise(words, scales, values):
             nc.vector.quantize_mx(out=words.bitcast(E4M3), scales=scales, in_=values)
 
-        def lay_w(a, cut):
+        def lay_w(a, cut, rest):
             laid = wk_in[a][:].rearrange("p (t m i) -> p m t i", t=PACK, i=PACK)
             raw = w_raw[a][:].rearrange("p i (m t) -> p m t i", t=PACK)
             nc.scalar.copy(out=laid[:, 0:cut], in_=raw[:, 0:cut])
-            if cut < P:
-                nc.gpsimd.tensor_scalar(laid[:, cut:P], raw[:, cut:P], 1.0, 0.0, MULT, ADD)
+            rest(laid[:, cut:P], raw[:, cut:P])
 
         def turn_w(a):
             pairs = wk_in[a][:].bitcast(F32)
@@ -285,11 +284,11 @@ def tile_list_tied_jet_gradient_kernel(
             if f == 0:
                 nc.sync.dma_start(idx2[:], offs2)
             nc.sync.dma_start(out=wgo_sb[:, cols(f)], in_=wgo[:, cols(f)])
-        lay_w(0, P // 2)
+        lay_w(0, P // 2, lambda laid, raw: nc.gpsimd.tensor_scalar(laid, raw, 1.0, 0.0, MULT, ADD))
         quantise(wk_w[0][:], wk_s[0][:], wk_in[0][:])
         turn_w(0)
         pick_s(0, picked_first[:], slice(0, S))
-        lay_w(1, 5 * P // 8)
+        lay_w(1, 3 * P // 8, nc.vector.tensor_copy)
         quantise(wr_w[0][:], wr_s[0][:], wr_in[0][:])
         quantise(wk_w[1][:], wk_s[1][:], wk_in[1][:])
         squares = held("w_raw1", [P, S], F32)

@@ -26,6 +26,7 @@ PASS = P * PACK
 HALF = 512
 QUARTER = 256
 PAGES = 3
+COPIED = 2
 PIECES = (slice(0, QUARTER), slice(QUARTER, HALF), slice(HALF, S))
 
 
@@ -65,7 +66,6 @@ def tile_list_tied_jet_gradient_kernel(
         wk_w = [held("wk_w%d" % a, [P, H], U32) for a in range(2)]
         wk_s = [held("wk_s%d" % a, [P, H], U8) for a in range(2)]
         wr_in = [held("wr_in%d" % a, [P, PACK * PASS], BF16) for a in range(2)]
-        wr_w = [held("wr_w0", [P, PASS], U32)]
         wr_s = [held("wr_s%d" % a, [P, PASS], U8) for a in range(2)]
         s_raw = [held("s_raw%d" % t, [P, T], F32) for t in range(PACK)]
         picked_first = held("picked_first", [P, S], F32)
@@ -74,8 +74,7 @@ def tile_list_tied_jet_gradient_kernel(
         early = [None, [held("early10", [P, HALF], F32)[:], picked[1][1]]]
         third = [held("third%d" % f, [P, HALF], F32) for f in range(2)]
         fourth = [held("fourth%d" % j, [P, width(part)], F32) for j, part in enumerate(PIECES)]
-        late = [[third[k // 2][:, quarter(k % 2)] for k in range(4)]]
-        late.append([fourth[min(k, 2)][:, quarter(k - min(k, 2))] for k in range(4)])
+        late = [[third[0][:, quarter(k)] for k in range(2)], [fourth[k][:] for k in range(2)]]
         h_sb = [[held("h_sb%d" % t, [P, HALF], F32)[:]] for t in range(2)]
         factor = [held("factor%d" % k, [P, 2 * QUARTER], F32) for k in range(2)]
         d_in = [held("d_in%d" % j, [P, PACK * width(part)], BF16) for j, part in enumerate(PIECES)]
@@ -91,7 +90,7 @@ def tile_list_tied_jet_gradient_kernel(
         wgo_sb = held("wgo_sb", [P, S], F32)
         ident = held("ident", [P, P], F32)
         pages = [held("page%d" % g, [P, T], F32) for g in range(PAGES)]
-        h_late = [ps_h.tile([P, 2 * QUARTER], F32, name="h_late%d" % k) for k in range(4)]
+        h_late = [ps_h.tile([P, 2 * QUARTER], F32, name="h_late%d" % k) for k in range(3)]
 
         nc.gpsimd.memset(tab_s[:].bitcast(I32), 0)
         nc.gpsimd.memset(gain_rows[:], 0.0)
@@ -122,12 +121,12 @@ def tile_list_tied_jet_gradient_kernel(
                 in_=tab_scales.bitcast(I32)[:, r:16:4, :].rearrange("a q n -> q a n"),
             )
         load_w(0, slice(0, PACK))
-        load_s(0, slice(0, T // 2))
-        load_s(0, slice(T // 2, T))
+        load_s(0, slice(0, T))
         load_w(1, slice(0, 2))
         load_w(1, slice(2, PACK))
         load_words(tab_w[1], tab_words[1], slice(0, T // 2))
         load_words(tab_w[1], tab_words[1], slice(T // 2, T))
+        nc.sync.dma_start(out=gain_rows[0 : N // P, :], in_=gain.rearrange("(b p) -> b p", p=P))
         nc.sync.dma_start(out=slope_sb[:], in_=slope.rearrange("(p t) -> p t", t=PACK))
 
         def pick_words(a, part):
@@ -208,9 +207,7 @@ def tile_list_tied_jet_gradient_kernel(
             if k == 0:
                 pairs = d_in[0][:].rearrange("p (c i e) -> p c e i", i=4, e=PACK)[:, :, 2:PACK, :]
             else:
-                j = min(k, 2)
-                first = 2 * width(PIECES[j]) + 2 * QUARTER * (k - j)
-                pairs = d_pairs[j][:, first : first + 2 * QUARTER].rearrange("p (c i u) -> p c u i", i=4, u=2)
+                pairs = d_pairs[k][:, HALF:S].rearrange("p (c i u) -> p c u i", i=4, u=2)
             nc.vector.tensor_tensor(
                 pairs,
                 h_late[k][:].rearrange("p (u c i) -> p c u i", u=2, i=4),
@@ -230,13 +227,11 @@ def tile_list_tied_jet_gradient_kernel(
             inside = slice(part.start - f * HALF, part.stop - f * HALF)
             quantise(d_w[f][:, inside], d_s[f][:, inside], d_in[j][:])
 
-        def make_y(b, part, y):
-            f = part.start // HALF
-            inside = slice(part.start - f * HALF, part.stop - f * HALF)
-            acc = ps_y.tile([P, HALF], F32, name="acc")
+        def open_y(b, part):
+            acc = ps_y.tile([P, HALF], F32, name="acc")[:, 0 : width(part)]
             for a in range(2):
                 nc.tensor.matmul_mx(
-                    out=acc[:, 0 : width(part)],
+                    out=acc,
                     lhsT=c_w[a][:, P * b : P * (b + 1)].bitcast(E4M3),
                     lhsT_scale=c_s[:, a, P * b : P * (b + 1)],
                     rhs=v_w[a][:, part].bitcast(E5M2),
@@ -244,9 +239,14 @@ def tile_list_tied_jet_gradient_kernel(
                     start=(a == 0),
                     stop=False,
                 )
+            return acc
+
+        def close_y(b, part, acc):
+            f = part.start // HALF
+            inside = slice(part.start - f * HALF, part.stop - f * HALF)
             a, j = divmod(b, PACK)
             nc.tensor.matmul_mx(
-                out=acc[:, 0 : width(part)],
+                out=acc,
                 lhsT=wr_w[a][:, P * j : P * (j + 1)].bitcast(E4M3),
                 lhsT_scale=wr_s[a][:, P * j : P * (j + 1)],
                 rhs=d_w[f][:, inside].bitcast(E4M3),
@@ -254,7 +254,13 @@ def tile_list_tied_jet_gradient_kernel(
                 start=False,
                 stop=True,
             )
-            nc.scalar.activation(y, acc[:, 0 : width(part)], COPY, scale=gain_sb[:, b : b + 1])
+            return acc
+
+        def sum_y(b, part):
+            return close_y(b, part, open_y(b, part))
+
+        def make_y(b, part, y):
+            nc.scalar.activation(y, sum_y(b, part), COPY, scale=gain_sb[:, b : b + 1])
 
         def place(b, y, part):
             nc.vector.tensor_tensor(
@@ -272,7 +278,7 @@ def tile_list_tied_jet_gradient_kernel(
         pick_scales()
         for t in range(1, PACK):
             load_s(t, slice(0, T))
-        nc.sync.dma_start(out=gain_rows[0 : N // P, :], in_=gain.rearrange("(b p) -> b p", p=P))
+        nc.sync.dma_start(out=wgo_sb[:, PIECES[0]], in_=wgo[:, PIECES[0]])
         for q in range(4):
             nc.sync.dma_start(
                 out=c_s[32 * q : 32 * q + 4, :, :].bitcast(I32),
@@ -283,12 +289,13 @@ def tile_list_tied_jet_gradient_kernel(
                 load_words(c_w[a], c_words[a], cols(f))
             if f == 0:
                 nc.sync.dma_start(idx2[:], offs2)
-            nc.sync.dma_start(out=wgo_sb[:, cols(f)], in_=wgo[:, cols(f)])
+        nc.sync.dma_start(out=wgo_sb[:, QUARTER:S], in_=wgo[:, QUARTER:S])
         lay_w(0, P // 2, lambda laid, raw: nc.gpsimd.tensor_scalar(laid, raw, 1.0, 0.0, MULT, ADD))
         quantise(wk_w[0][:], wk_s[0][:], wk_in[0][:])
         turn_w(0)
         pick_s(0, picked_first[:], slice(0, S))
         lay_w(1, 3 * P // 8, nc.vector.tensor_copy)
+        wr_w = [held("wr_w0", [P, PASS], U32)]
         quantise(wr_w[0][:], wr_s[0][:], wr_in[0][:])
         quantise(wk_w[1][:], wk_s[1][:], wk_in[1][:])
         squares = held("w_raw1", [P, S], F32)
@@ -298,6 +305,10 @@ def tile_list_tied_jet_gradient_kernel(
         turn_w(1)
         for f in range(2):
             pick_words(1, cols(f))
+        gain_bank = ps_h.tile([P, HALF], F32, name="h_late3")
+        nc.tensor.transpose(gain_bank[:, 0:P], gain_rows[:], ident[:])
+        nc.scalar.copy(out=gain_sb[:], in_=gain_bank[:, 0 : N // P])
+        h_late.append(ps_h.tile([P, 2 * QUARTER], F32, name="h_late3"))
         nc.scalar.activation(minus_slope[:], slope_sb[:], COPY, scale=-1.0)
         for t in range(2):
             empty_h(t, 0)
@@ -314,12 +325,11 @@ def tile_list_tied_jet_gradient_kernel(
         early_d(0, 2)
         early_factor(1, 1)
         early_d(1, 2)
-        for k in range(4):
+        for k in range(2):
             for u in range(2):
                 sum_h(h_late[k][:, quarter(u)], 2 + u, quarter(k))
-        gain_bank = ps_y.tile([P, HALF], F32, name="acc")
-        nc.tensor.transpose(gain_bank[:, 0:P], gain_rows[:], ident[:])
-        nc.scalar.copy(out=gain_sb[:], in_=gain_bank[:, 0 : N // P])
+        for u in range(2):
+            sum_h(h_late[2 + u][:], 2 + u, cols(1))
         for f in range(2):
             pick_s(2, third[f][:], cols(f))
         for j, part in enumerate(PIECES):
@@ -335,33 +345,45 @@ def tile_list_tied_jet_gradient_kernel(
         late_factor(1, 1)
         late_d(1)
         quantise_d(0)
-        for k in range(2, 4):
-            factor.append(held(("early10", "fourth1")[k - 2], [P, 2 * QUARTER], F32))
-            late_factor(0, k)
         wr_w.append(held("d_in0", [P, PASS], U32))
         quantise(wr_w[1][:], wr_s[1][:], wr_in[1][:])
-
-        def first_piece(b, name):
-            y = held(name, [P, QUARTER], F32)
-            make_y(b, PIECES[0], y[:])
-            place(b, y[:], PIECES[0])
-
-        first_piece(0, "y_first")
-        for k in range(2, 4):
-            late_square(k)
-            late_factor(1, k)
-            late_d(k)
+        weights = held("early10", [P, COPIED * QUARTER], F32)
+        weight = [weights[:, quarter(b)] for b in range(COPIED)]
+        for b in range(COPIED):
+            nc.scalar.activation(weight[b], wgo_sb[:, PIECES[0]], COPY, scale=gain_sb[:, b : b + 1])
         lay_d(1)
         quantise_d(1)
-        first_piece(1, "early10")
+        weighed = [held("weighed%d" % b, [P, QUARTER], F32) for b in range(COPIED)]
+        opened = [open_y(b, PIECES[0]) for b in range(COPIED)]
+        for b in range(COPIED):
+            nc.vector.tensor_tensor(weighed[b][:], close_y(b, PIECES[0], opened[b]), weight[b], MULT)
+        for b in range(COPIED):
+            nc.vector.tensor_copy(pages[b][:].indirect(idx2[:, entries(PIECES[0])]), weighed[b][:])
+        rest_both = held("d_pairs1", [P, S], F32)
+        rest = [rest_both[:, cols(u)] for u in range(2)]
+        nc.scalar.activation(rest[0], third[1][:], COPY, bias=-1.0, scale=1.0)
+        h_rest = held("wr_in1", [P, S], F32)
+        for u in range(2):
+            if u == 1:
+                nc.scalar.activation(rest[1], fourth[2][:], SQUARE)
+                nc.scalar.activation(rest[1], rest[1], COPY, bias=-1.0, scale=1.0)
+            nc.scalar.activation(h_rest[:, cols(u)], h_late[2 + u][:], COPY, scale=minus_slope[:, 2 + u : 3 + u])
+            pairs = d_pairs[2][:, S : 2 * S].rearrange("p (c e) -> p c e", e=2)
+            nc.gpsimd.tensor_tensor(pairs[:, :, u], h_rest[:, cols(u)], rest[u], MULT)
+        first = [yring.tile([P, S], F32, name="y") for b in range(PAGES)]
+        make_y(0, PIECES[1], first[0][:, PIECES[1]])
+        place(0, first[0][:, PIECES[1]], PIECES[1])
         lay_d(2)
         quantise_d(2)
-        first_piece(2, "d_pairs2")
+        y_third = held("d_pairs2", [P, QUARTER], F32)
+        make_y(2, PIECES[0], y_third[:])
+        place(2, y_third[:], PIECES[0])
         for b in range(PAGES):
-            y = yring.tile([P, S], F32, name="y")
-            for part in PIECES[1:]:
-                make_y(b, part, y[:, part])
-            place(b, y[:, QUARTER:S], slice(QUARTER, S))
+            parts = PIECES[2:] if b == 0 else PIECES[1:]
+            for part in parts:
+                make_y(b, part, first[b][:, part])
+            left = slice(parts[0].start, S)
+            place(b, first[b][:, left], left)
             store(b)
         for b in range(PAGES, N // P):
             y = yring.tile([P, S], F32, name="y")

@@ -345,7 +345,7 @@ def tile_list_tied_jet_gradient_kernel(
         late_factor(1, 1)
         late_d(1)
         quantise_d(0)
-        wr_w.append(held("d_in0", [P, PASS], U32))
+        wr_w.append(held("factor1", [P, PASS], U32))
         quantise(wr_w[1][:], wr_s[1][:], wr_in[1][:])
         weights = held("early10", [P, COPIED * QUARTER], F32)
         weight = [weights[:, quarter(b)] for b in range(COPIED)]
@@ -362,7 +362,7 @@ def tile_list_tied_jet_gradient_kernel(
         rest_both = held("d_pairs1", [P, S], F32)
         rest = [rest_both[:, cols(u)] for u in range(2)]
         nc.scalar.activation(rest[0], third[1][:], COPY, bias=-1.0, scale=1.0)
-        h_rest = held("wr_in1", [P, S], F32)
+        h_rest = held("d_in0", [P, S], F32)
         for u in range(2):
             if u == 1:
                 nc.scalar.activation(rest[1], fourth[2][:], SQUARE)

@@ -41,7 +41,7 @@ def tile_list_tied_jet_gradient_kernel(
         ps_y = ctx.enter_context(tc.psum_pool(name="ps_y", bufs=4))
 
         def held(name, shape, dtype):
-            return keep.tile(shape, dtype, name=name, align_bytes=64)
+            return keep.tile(shape, dtype, name=name, align_bytes=256)
 
         def width(part):
             return part.stop - part.start

@@ -28,6 +28,7 @@ QUARTER = 256
 PAGES = 3
 COPIED = 2
 PIECES = (slice(0, QUARTER), slice(QUARTER, HALF), slice(HALF, S))
+LAST_CUTS = PIECES[:2] + (slice(HALF, S - P), slice(S - P, S))
 
 
 def tile_list_tied_jet_gradient_kernel(
@@ -38,7 +39,7 @@ def tile_list_tied_jet_gradient_kernel(
         keep = ctx.enter_context(tc.tile_pool(name="keep", bufs=1))
         yring = ctx.enter_context(tc.tile_pool(name="yring", bufs=PAGES + 1))
         ps_h = ctx.enter_context(tc.psum_pool(name="ps_h", bufs=1))
-        ps_y = ctx.enter_context(tc.psum_pool(name="ps_y", bufs=4))
+        ps_y = ctx.enter_context(tc.psum_pool(name="ps_y", bufs=3))
 
         def held(name, shape, dtype):
             return keep.tile(shape, dtype, name=name, align_bytes=256)
@@ -71,12 +72,13 @@ def tile_list_tied_jet_gradient_kernel(
         picked_first = held("picked_first", [P, S], F32)
         picked = [[picked_first[:, cols(f)] for f in range(2)]]
         picked.append([held("picked1%d" % f, [P, HALF], F32)[:] for f in range(2)])
-        early = [None, [held("early10", [P, HALF], F32)[:], picked[1][1]]]
+        early = held("early", [P, HALF], F32)
         third = [held("third%d" % f, [P, HALF], F32) for f in range(2)]
-        fourth = [held("fourth%d" % j, [P, width(part)], F32) for j, part in enumerate(PIECES)]
-        late = [[third[0][:, quarter(k)] for k in range(2)], [fourth[k][:] for k in range(2)]]
-        h_sb = [[held("h_sb%d" % t, [P, HALF], F32)[:]] for t in range(2)]
-        factor = [held("factor%d" % k, [P, 2 * QUARTER], F32) for k in range(2)]
+        fourth = [held("fourth%d" % k, [P, width(part)], F32) for k, part in enumerate(LAST_CUTS[:3])]
+        h_early = held("h_early", [P, 2 * QUARTER], F32)
+        h_zero = held("h_zero", [P, HALF], F32)
+        factor = held("factor", [P, PACK, QUARTER], F32)
+        h_two = held("h_two", [P, QUARTER], F32)
         d_in = [held("d_in%d" % j, [P, PACK * width(part)], BF16) for j, part in enumerate(PIECES)]
         d_pairs = [d_in[0]] + [held("d_pairs%d" % j, [P, PACK * width(PIECES[j])], BF16) for j in range(1, 3)]
         d_w = [held("d_w%d" % f, [P, HALF], U32) for f in range(2)]
@@ -90,7 +92,9 @@ def tile_list_tied_jet_gradient_kernel(
         wgo_sb = held("wgo_sb", [P, S], F32)
         ident = held("ident", [P, P], F32)
         pages = [held("page%d" % g, [P, T], F32) for g in range(PAGES)]
-        h_late = [ps_h.tile([P, 2 * QUARTER], F32, name="h_late%d" % k) for k in range(3)]
+        h_first = [ps_h.tile([P, PACK, P], F32, name="h_first%d" % k) for k in range(2)]
+        h_second = ps_h.tile([P, 2 * QUARTER], F32, name="h_second")
+        h_rest = [ps_h.tile([P, HALF], F32, name="h_rest0")]
 
         nc.gpsimd.memset(tab_s[:].bitcast(I32), 0)
         nc.gpsimd.memset(gain_rows[:], 0.0)
@@ -173,47 +177,32 @@ def tile_list_tied_jet_gradient_kernel(
                     stop=(a == 1),
                 )
 
-        def empty_h(t, f):
-            h = ps_y.tile([P, HALF], F32, name="acc")
-            sum_h(h[:], t, cols(f))
-            nc.scalar.activation(h_sb[t][f], h[:], COPY, scale=minus_slope[:, t : t + 1])
+        def empty_h(target, bank, t):
+            nc.scalar.activation(target, bank, COPY, scale=minus_slope[:, t : t + 1])
 
-        def early_d(t, j):
-            part = PIECES[j]
-            f = part.start // HALF
-            inside = slice(part.start - f * HALF, part.stop - f * HALF)
-            if j == 0:
-                pairs = d_in[0][:].rearrange("p (c e) -> p c e", e=PACK)
-            else:
-                pairs = d_pairs[j][:, 0 : 2 * width(part)].rearrange("p (c e) -> p c e", e=2)
-            nc.gpsimd.tensor_tensor(pairs[:, :, t], h_sb[t][f][:, inside], early[t][f][:, inside], MULT)
-
-        def late_square(k):
-            values = late[1][k]
-            if k == 0:
-                late[1][k] = held("early10", [P, QUARTER], F32)[:]
-            nc.scalar.activation(late[1][k], values, SQUARE)
-
-        def late_factor(u, k):
+        def first_factor(t, square):
             nc.scalar.activation(
-                factor[k][:, quarter(u)],
-                late[u][k],
-                IDENTITY,
-                scale=minus_slope[:, 2 + u : 3 + u],
-                bias=slope_sb[:, 2 + u : 3 + u],
+                factor[:, t], square, IDENTITY, scale=minus_slope[:, t : t + 1], bias=slope_sb[:, t : t + 1]
             )
 
-        def late_d(k):
-            if k == 0:
-                pairs = d_in[0][:].rearrange("p (c i e) -> p c e i", i=4, e=PACK)[:, :, 2:PACK, :]
-            else:
-                pairs = d_pairs[k][:, HALF:S].rearrange("p (c i u) -> p c u i", i=4, u=2)
+        def less_one(values):
+            nc.scalar.activation(values, values, COPY, bias=-1.0, scale=1.0)
+
+        def less_one_aside(values):
+            nc.gpsimd.tensor_scalar(values, values, 1.0, -1.0, MULT, ADD)
+
+        def first_d(k):
             nc.vector.tensor_tensor(
-                pairs,
-                h_late[k][:].rearrange("p (u c i) -> p c u i", u=2, i=4),
-                factor[k][:].rearrange("p (u c i) -> p c u i", u=2, i=4),
+                d_in[0][:, PASS * k : PASS * (k + 1)].rearrange("p (c i e) -> p c e i", i=4, e=PACK),
+                h_first[k][:].rearrange("p t (c i) -> p c t i", i=4),
+                factor[:, :, P * k : P * (k + 1)].rearrange("p t (c i) -> p c t i", i=4),
                 MULT,
             )
+
+        def pair_d(j, t, h, values):
+            n = 2 * width(PIECES[j])
+            pairs = d_pairs[j][:, n * (t // 2) : n * (t // 2 + 1)].rearrange("p (c e) -> p c e", e=2)
+            nc.gpsimd.tensor_tensor(pairs[:, :, t % 2], h, values, MULT)
 
         def lay_d(j):
             nc.scalar.copy(
@@ -270,10 +259,6 @@ def tile_list_tied_jet_gradient_kernel(
         def store(b):
             nc.sync.dma_start(out=out[P * b : P * (b + 1), :], in_=pages[b % PAGES][:])
 
-        def early_factor(t, f):
-            nc.scalar.activation(early[t][f], picked[t][f], SQUARE)
-            nc.gpsimd.tensor_scalar(early[t][f], early[t][f], 1.0, -1.0, MULT, ADD)
-
         pick_words(0, slice(0, S))
         pick_scales()
         for t in range(1, PACK):
@@ -299,58 +284,78 @@ def tile_list_tied_jet_gradient_kernel(
         quantise(wr_w[0][:], wr_s[0][:], wr_in[0][:])
         quantise(wk_w[1][:], wk_s[1][:], wk_in[1][:])
         squares = held("w_raw1", [P, S], F32)
-        early[0] = [squares[:, cols(f)] for f in range(2)]
         for f in range(2):
-            early_factor(0, f)
+            nc.scalar.activation(squares[:, cols(f)], picked[0][f], SQUARE)
+        less_one_aside(squares[:, QUARTER:S])
         turn_w(1)
         for f in range(2):
             pick_words(1, cols(f))
-        gain_bank = ps_h.tile([P, HALF], F32, name="h_late3")
+        gain_bank = ps_h.tile([P, HALF], F32, name="h_rest1")
         nc.tensor.transpose(gain_bank[:, 0:P], gain_rows[:], ident[:])
         nc.scalar.copy(out=gain_sb[:], in_=gain_bank[:, 0 : N // P])
-        h_late.append(ps_h.tile([P, 2 * QUARTER], F32, name="h_late3"))
+        h_rest.append(ps_h.tile([P, HALF], F32, name="h_rest1"))
         nc.scalar.activation(minus_slope[:], slope_sb[:], COPY, scale=-1.0)
+        first_factor(0, squares[:, quarter(0)])
+        bank = ps_y.tile([P, HALF], F32, name="acc")
         for t in range(2):
-            empty_h(t, 0)
+            sum_h(bank[:, quarter(t)], t, quarter(1))
+        for t in range(2):
+            empty_h(h_early[:, quarter(t)], bank[:, quarter(t)], t)
+        pair_d(1, 0, h_early[:, quarter(0)], squares[:, quarter(1)])
+        bank = ps_y.tile([P, HALF], F32, name="acc")
+        sum_h(bank[:], 0, cols(1))
+        empty_h(h_zero[:], bank[:], 0)
+        pair_d(2, 0, h_zero[:], squares[:, cols(1)])
         for f in range(2):
             pick_s(1, picked[1][f], cols(f))
-        early_factor(1, 0)
-        for t in range(2):
-            for j in range(2):
-                early_d(t, j)
-        h_second = held("picked10", [P, S], F32)
-        for t in range(2):
-            h_sb[t].append(h_second[:, cols(t)])
-            empty_h(t, 1)
-        early_d(0, 2)
-        early_factor(1, 1)
-        early_d(1, 2)
-        for k in range(2):
-            for u in range(2):
-                sum_h(h_late[k][:, quarter(u)], 2 + u, quarter(k))
+        nc.scalar.activation(early[:], picked[1][0], SQUARE)
+        first_factor(1, early[:, quarter(0)])
+        less_one_aside(early[:, quarter(1)])
+        pair_d(1, 1, h_early[:, quarter(1)], early[:, quarter(1)])
+        h_one = held("picked10", [P, HALF], F32)
+        bank = ps_y.tile([P, HALF], F32, name="acc")
+        sum_h(bank[:], 1, cols(1))
+        empty_h(h_one[:], bank[:], 1)
+        nc.scalar.activation(picked[1][1], picked[1][1], SQUARE)
+        less_one_aside(picked[1][1])
+        pair_d(2, 1, h_one[:], picked[1][1])
         for u in range(2):
-            sum_h(h_late[2 + u][:], 2 + u, cols(1))
+            sum_h(h_second[:, quarter(u)], 2 + u, quarter(1))
+        for k in range(2):
+            for t in range(PACK):
+                sum_h(h_first[k][:, t], t, slice(P * k, P * (k + 1)))
+        for u in range(2):
+            sum_h(h_rest[u][:], 2 + u, cols(1))
         for f in range(2):
             pick_s(2, third[f][:], cols(f))
-        for j, part in enumerate(PIECES):
-            pick_s(3, fourth[j][:], part)
+        for k in range(3):
+            pick_s(3, fourth[k][:], LAST_CUTS[k])
         nc.scalar.activation(third[0][:], third[0][:], SQUARE)
+        first_factor(2, third[0][:, quarter(0)])
+        less_one(third[0][:, quarter(1)])
+        empty_h(h_two[:], h_second[:, quarter(0)], 2)
+        pair_d(1, 2, h_two[:], third[0][:, quarter(1)])
+        chain_square = held("chain_square", [P, QUARTER], F32)
+        nc.scalar.activation(chain_square[:], fourth[0][:], SQUARE)
+        first_factor(3, chain_square[:])
         for k in range(2):
-            late_factor(0, k)
-        nc.scalar.activation(third[1][:], third[1][:], SQUARE)
-        late_square(0)
-        late_factor(1, 0)
-        late_d(0)
-        late_square(1)
-        late_factor(1, 1)
-        late_d(1)
-        quantise_d(0)
-        wr_w.append(held("factor1", [P, PASS], U32))
-        quantise(wr_w[1][:], wr_s[1][:], wr_in[1][:])
-        weights = held("early10", [P, COPIED * QUARTER], F32)
-        weight = [weights[:, quarter(b)] for b in range(COPIED)]
+            first_d(k)
+        fourth.append(held("chain_square", [P, P], F32))
+        pick_s(3, fourth[3][:], LAST_CUTS[3])
+        behind = held("fourth0", [P, HALF + (1 + COPIED) * QUARTER], F32)
+        h_three, third_rest = behind[:, quarter(0)], behind[:, QUARTER : QUARTER + HALF]
+        empty_h(h_three, h_second[:, quarter(1)], 3)
+        nc.scalar.activation(fourth[1][:], fourth[1][:], SQUARE)
+        less_one(fourth[1][:])
+        pair_d(1, 3, h_three, fourth[1][:])
+        weight = [behind[:, quarter(3 + b)] for b in range(COPIED)]
         for b in range(COPIED):
             nc.scalar.activation(weight[b], wgo_sb[:, PIECES[0]], COPY, scale=gain_sb[:, b : b + 1])
+        quantise_d(0)
+        wr_w.append(held("factor", [P, PASS], U32))
+        quantise(wr_w[1][:], wr_s[1][:], wr_in[1][:])
+        nc.scalar.activation(third_rest, third[1][:], SQUARE)
+        less_one(third_rest)
         lay_d(1)
         quantise_d(1)
         weighed = [held("weighed%d" % b, [P, QUARTER], F32) for b in range(COPIED)]
@@ -359,27 +364,27 @@ def tile_list_tied_jet_gradient_kernel(
             nc.vector.tensor_tensor(weighed[b][:], close_y(b, PIECES[0], opened[b]), weight[b], MULT)
         for b in range(COPIED):
             nc.vector.tensor_copy(pages[b][:].indirect(idx2[:, entries(PIECES[0])]), weighed[b][:])
-        rest_both = held("d_pairs1", [P, S], F32)
-        rest = [rest_both[:, cols(u)] for u in range(2)]
-        nc.scalar.activation(rest[0], third[1][:], COPY, bias=-1.0, scale=1.0)
-        h_rest = held("d_in0", [P, S], F32)
-        for u in range(2):
-            if u == 1:
-                nc.scalar.activation(rest[1], fourth[2][:], SQUARE)
-                nc.scalar.activation(rest[1], rest[1], COPY, bias=-1.0, scale=1.0)
-            nc.scalar.activation(h_rest[:, cols(u)], h_late[2 + u][:], COPY, scale=minus_slope[:, 2 + u : 3 + u])
-            pairs = d_pairs[2][:, S : 2 * S].rearrange("p (c e) -> p c e", e=2)
-            nc.gpsimd.tensor_tensor(pairs[:, :, u], h_rest[:, cols(u)], rest[u], MULT)
+        rest = held("d_pairs1", [P, 3, HALF], F32)
+        empty_h(rest[:, 0], h_rest[0][:], 2)
+        pair_d(2, 2, rest[:, 0], third_rest)
+        for k in range(2):
+            part = LAST_CUTS[2 + k]
+            nc.scalar.activation(rest[:, 1, part.start - HALF : part.stop - HALF], fourth[2 + k][:], SQUARE)
+        less_one(rest[:, 1])
+        empty_h(rest[:, 2], h_rest[1][:], 3)
+        pair_d(2, 3, rest[:, 2], rest[:, 1])
         first = [yring.tile([P, S], F32, name="y") for b in range(PAGES)]
         make_y(0, PIECES[1], first[0][:, PIECES[1]])
         place(0, first[0][:, PIECES[1]], PIECES[1])
+        make_y(1, PIECES[1], first[1][:, PIECES[1]])
+        place(1, first[1][:, PIECES[1]], PIECES[1])
         lay_d(2)
         quantise_d(2)
         y_third = held("d_pairs2", [P, QUARTER], F32)
         make_y(2, PIECES[0], y_third[:])
         place(2, y_third[:], PIECES[0])
         for b in range(PAGES):
-            parts = PIECES[2:] if b == 0 else PIECES[1:]
+            parts = PIECES[2:] if b < COPIED else PIECES[1:]
             for part in parts:
                 make_y(b, part, first[b][:, part])
             left = slice(parts[0].start, S)

@@ -342,15 +342,14 @@ def tile_list_tied_jet_gradient_kernel(
             first_d(k)
         fourth.append(held("chain_square", [P, P], F32))
         pick_s(3, fourth[3][:], LAST_CUTS[3])
-        behind = held("fourth0", [P, HALF + (1 + COPIED) * QUARTER], F32)
+        behind = held("fourth0", [P, HALF + QUARTER], F32)
         h_three, third_rest = behind[:, quarter(0)], behind[:, QUARTER : QUARTER + HALF]
         empty_h(h_three, h_second[:, quarter(1)], 3)
         nc.scalar.activation(fourth[1][:], fourth[1][:], SQUARE)
         less_one(fourth[1][:])
         pair_d(1, 3, h_three, fourth[1][:])
-        weight = [behind[:, quarter(3 + b)] for b in range(COPIED)]
-        for b in range(COPIED):
-            nc.scalar.activation(weight[b], wgo_sb[:, PIECES[0]], COPY, scale=gain_sb[:, b : b + 1])
+        weight = held("weight", [P, QUARTER], F32)
+        nc.scalar.activation(weight[:], wgo_sb[:, PIECES[0]], COPY, scale=gain_sb[:, 0:1])
         quantise_d(0)
         wr_w.append(held("factor", [P, PASS], U32))
         quantise(wr_w[1][:], wr_s[1][:], wr_in[1][:])
@@ -358,31 +357,34 @@ def tile_list_tied_jet_gradient_kernel(
         less_one(third_rest)
         lay_d(1)
         quantise_d(1)
-        weighed = [held("weighed%d" % b, [P, QUARTER], F32) for b in range(COPIED)]
-        opened = [open_y(b, PIECES[0]) for b in range(COPIED)]
-        for b in range(COPIED):
-            nc.vector.tensor_tensor(weighed[b][:], close_y(b, PIECES[0], opened[b]), weight[b], MULT)
-        for b in range(COPIED):
+        weighed = [held("weighed%d" % b, [P, QUARTER], F32) for b in range(PAGES)]
+        opened = [open_y(b, PIECES[0]) for b in range(PAGES)]
+        nc.vector.tensor_tensor(weighed[0][:], close_y(0, PIECES[0], opened[0]), weight[:], MULT)
+        for b in range(1, PAGES):
+            y = held("y_first%d" % b, [P, QUARTER], F32)
+            nc.scalar.activation(y[:], close_y(b, PIECES[0], opened[b]), COPY, scale=gain_sb[:, b : b + 1])
+            nc.gpsimd.tensor_tensor(weighed[b][:], y[:], wgo_sb[:, PIECES[0]], MULT)
+        for b in range(PAGES):
             nc.vector.tensor_copy(pages[b][:].indirect(idx2[:, entries(PIECES[0])]), weighed[b][:])
-        rest = held("d_pairs1", [P, 3, HALF], F32)
-        empty_h(rest[:, 0], h_rest[0][:], 2)
-        pair_d(2, 2, rest[:, 0], third_rest)
+        h_two_rest = held("y_first1", [P, HALF], F32)
+        empty_h(h_two_rest[:], h_rest[0][:], 2)
+        pair_d(2, 2, h_two_rest[:], third_rest)
+        last = held("weight", [P, HALF], F32)
         for k in range(2):
             part = LAST_CUTS[2 + k]
-            nc.scalar.activation(rest[:, 1, part.start - HALF : part.stop - HALF], fourth[2 + k][:], SQUARE)
-        less_one(rest[:, 1])
-        empty_h(rest[:, 2], h_rest[1][:], 3)
-        pair_d(2, 3, rest[:, 2], rest[:, 1])
+            nc.scalar.activation(last[:, part.start - HALF : part.stop - HALF], fourth[2 + k][:], SQUARE)
+        less_one(last[:])
+        h_last = held("y_first2", [P, HALF], F32)
+        empty_h(h_last[:], h_rest[1][:], 3)
+        pair_d(2, 3, h_last[:], last[:])
         first = [yring.tile([P, S], F32, name="y") for b in range(PAGES)]
         make_y(0, PIECES[1], first[0][:, PIECES[1]])
         place(0, first[0][:, PIECES[1]], PIECES[1])
-        make_y(1, PIECES[1], first[1][:, PIECES[1]])
-        place(1, first[1][:, PIECES[1]], PIECES[1])
         lay_d(2)
         quantise_d(2)
-        y_third = held("d_pairs2", [P, QUARTER], F32)
-        make_y(2, PIECES[0], y_third[:])
-        place(2, y_third[:], PIECES[0])
+        y_second = held("d_pairs2", [P, QUARTER], F32)
+        make_y(1, PIECES[1], y_second[:])
+        place(1, y_second[:], PIECES[1])
         for b in range(PAGES):
             parts = PIECES[2:] if b < COPIED else PIECES[1:]
             for part in parts:

@@ -262,7 +262,8 @@ def tile_list_tied_jet_gradient_kernel(
         pick_words(0, slice(0, S))
         pick_scales()
         for t in range(1, PACK):
-            load_s(t, slice(0, T))
+            for part in (slice(0, T // 2), slice(T // 2, T)):
+                load_s(t, part)
         nc.sync.dma_start(out=wgo_sb[:, PIECES[0]], in_=wgo[:, PIECES[0]])
         for q in range(4):
             nc.sync.dma_start(

from contextlib import ExitStack

import concourse.mybir as mybir
from concourse.masks import make_identity

K, H, N, T, S = 1024, 512, 1024, 2048, 1024
FLOPS = 2 * S * (K * H + H * N + K * N)

F32 = mybir.dt.float32
BF16 = mybir.dt.bfloat16
I32 = mybir.dt.int32
U32 = mybir.dt.uint32
U16 = mybir.dt.uint16
U8 = mybir.dt.uint8
E4M3 = mybir.dt.float8_e4m3fn_x4
E5M2 = mybir.dt.float8_e5m2_x4
MULT = mybir.AluOpType.mult
ADD = mybir.AluOpType.add
COPY = mybir.ActivationFunctionType.Copy
IDENTITY = mybir.ActivationFunctionType.Identity
SQUARE = mybir.ActivationFunctionType.Square

P = 128
PACK = 4
PASS = P * PACK
HALF = 512
QUARTER = 256
PAGES = 3
COPIED = 2
PIECES = (slice(0, QUARTER), slice(QUARTER, HALF), slice(HALF, S))
LAST_CUTS = PIECES[:2] + (slice(HALF, S - P), slice(S - P, S))


def tile_list_tied_jet_gradient_kernel(
    tc, tab_words, tab_scales, offs, offs2, sT, w, slope, c_words, c_scales, gain, wgo, out
):
    nc = tc.nc
    with ExitStack() as ctx:
        keep = ctx.enter_context(tc.tile_pool(name="keep", bufs=1))
        yring = ctx.enter_context(tc.tile_pool(name="yring", bufs=PAGES + 1))
        ps_h = ctx.enter_context(tc.psum_pool(name="ps_h", bufs=1))
        ps_y = ctx.enter_context(tc.psum_pool(name="ps_y", bufs=3))

        def held(name, shape, dtype):
            return keep.tile(shape, dtype, name=name, align_bytes=256)

        def width(part):
            return part.stop - part.start

        def cols(f):
            return slice(f * HALF, (f + 1) * HALF)

        def quarter(k):
            return slice(k * QUARTER, (k + 1) * QUARTER)

        def entries(part):
            return slice(part.start // 16, part.stop // 16)

        idx = keep.tile([P, S // 16], U16, name="idx")
        idx2 = keep.tile([P, S // 16], U16, name="idx2")
        tab_w = [held("tab_w%d" % a, [P, T], U32) for a in range(2)]
        tab_s = held("tab_s", [P, T], U8)
        v_w = [held("v_w%d" % a, [P, S], U32) for a in range(2)]
        v_s = [held("v_s%d" % a, [P, S], U8) for a in range(2)]
        w_raw = [held("w_raw%d" % a, [P, PACK, H], F32) for a in range(2)]
        wk_in = [held("wk_in%d" % a, [P, PACK * H], BF16) for a in range(2)]
        wk_w = [held("wk_w%d" % a, [P, H], U32) for a in range(2)]
        wk_s = [held("wk_s%d" % a, [P, H], U8) for a in range(2)]
        wr_in = [held("wr_in%d" % a, [P, PACK * PASS], BF16) for a in range(2)]
        wr_s = [held("wr_s%d" % a, [P, PASS], U8) for a in range(2)]
        s_raw = [held("s_raw%d" % t, [P, T], F32) for t in range(PACK)]
        picked_first = held("picked_first", [P, S], F32)
        picked = [[picked_first[:, cols(f)] for f in range(2)]]
        picked.append([held("picked1%d" % f, [P, HALF], F32)[:] for f in range(2)])
        early = held("early", [P, HALF], F32)
        third = [held("third%d" % f, [P, HALF], F32) for f in range(2)]
        fourth = [held("fourth%d" % k, [P, width(part)], F32) for k, part in enumerate(LAST_CUTS[:3])]
        h_early = held("h_early", [P, 2 * QUARTER], F32)
        h_zero = held("h_zero", [P, HALF], F32)
        factor = held("factor", [P, PACK, QUARTER], F32)
        h_two = held("h_two", [P, QUARTER], F32)
        d_in = [held("d_in%d" % j, [P, PACK * width(part)], BF16) for j, part in enumerate(PIECES)]
        d_pairs = [d_in[0]] + [held("d_pairs%d" % j, [P, PACK * width(PIECES[j])], BF16) for j in range(1, 3)]
        d_w = [held("d_w%d" % f, [P, HALF], U32) for f in range(2)]
        d_s = [held("d_s%d" % f, [P, HALF], U8) for f in range(2)]
        c_w = [held("c_w%d" % a, [P, N], U32) for a in range(2)]
        c_s = held("c_s", [P, 2, N], U8)
        slope_sb = held("slope_sb", [P, PACK], F32)
        minus_slope = held("minus_slope", [P, PACK], F32)
        gain_rows = held("gain_rows", [P, P], F32)
        gain_sb = held("gain_sb", [P, N // P], F32)
        wgo_sb = held("wgo_sb", [P, S], F32)
        ident = held("ident", [P, P], F32)
        pages = [held("page%d" % g, [P, T], F32) for g in range(PAGES)]
        h_first = [ps_h.tile([P, PACK, P], F32, name="h_first%d" % k) for k in range(2)]
        h_second = ps_h.tile([P, 2 * QUARTER], F32, name="h_second")
        h_rest = [ps_h.tile([P, HALF], F32, name="h_rest0")]

        nc.gpsimd.memset(tab_s[:].bitcast(I32), 0)
        nc.gpsimd.memset(gain_rows[:], 0.0)
        nc.gpsimd.memset(v_s[1][:].bitcast(I32), 0)
        make_identity(nc, ident[:])
        nc.gpsimd.memset(c_s[:].bitcast(I32), 0)
        for page in pages[:-1]:
            nc.vector.memset(page[:], 0.0)
        nc.gpsimd.memset(pages[-1][:], 0.0)

        def load_words(tile, words, part):
            nc.sync.dma_start(
                out=tile[:, part].bitcast(I32), in_=words.rearrange("p t i -> p (t i)").bitcast(I32)[:, part]
            )

        def load_w(a, part):
            rows = w[PASS * a : PASS * (a + 1), :].rearrange("(p i) r -> p i r", i=PACK)
            nc.sync.dma_start(out=w_raw[a][:, part], in_=rows[:, part])

        def load_s(t, part):
            nc.sync.dma_start(out=s_raw[t][:, part], in_=sT.rearrange("(p t) x -> p t x", t=PACK)[:, t, part])

        load_words(tab_w[0], tab_words[0], slice(0, T))
        nc.sync.dma_start(idx[:], offs)
        for r in range(4):
            nc.sync.dma_start(
                out=tab_s[r:P:16, :].bitcast(I32),
                in_=tab_scales.bitcast(I32)[:, r:16:4, :].rearrange("a q n -> q a n"),
            )
        load_w(0, slice(0, PACK))
        load_s(0, slice(0, T))
        load_w(1, slice(0, 2))
        load_w(1, slice(2, PACK))
        load_words(tab_w[1], tab_words[1], slice(0, T // 2))
        load_words(tab_w[1], tab_words[1], slice(T // 2, T))
        nc.sync.dma_start(out=gain_rows[0 : N // P, :], in_=gain.rearrange("(b p) -> b p", p=P))
        nc.sync.dma_start(out=slope_sb[:], in_=slope.rearrange("(p t) -> p t", t=PACK))

        def pick_words(a, part):
            nc.vector.tensor_copy(v_w[a][:, part], tab_w[a][:].indirect(idx[:, entries(part)]))

        def pick_scales():
            nc.vector.tensor_copy(v_s[0][:], tab_s[:].indirect(idx[:]))
            nc.sync.dma_start(out=v_s[1][0:112, :].bitcast(I32), in_=v_s[0][16:128, :].bitcast(I32))

        def quantise(words, scales, values):
            nc.vector.quantize_mx(out=words.bitcast(E4M3), scales=scales, in_=values)

        def lay_w(a, cut, rest):
            laid = wk_in[a][:].rearrange("p (t m i) -> p m t i", t=PACK, i=PACK)
            raw = w_raw[a][:].rearrange("p i (m t) -> p m t i", t=PACK)
            nc.scalar.copy(out=laid[:, 0:cut], in_=raw[:, 0:cut])
            rest(laid[:, cut:P], raw[:, cut:P])

        def turn_w(a):
            pairs = wk_in[a][:].bitcast(F32)
            for u in range(2):
                bank = ps_y.tile([P, HALF], F32, name="acc")
                for t in range(PACK):
                    nc.tensor.transpose(
                        bank[:, P * t : P * (t + 1)], pairs[:, 2 * P * t + u : 2 * P * (t + 1) : 2], ident[:]
                    )
                nc.scalar.copy(
                    out=wr_in[a][:].rearrange("m (p z u e t) -> m u p t z e", z=2, u=2, e=2, t=PACK)[:, u],
                    in_=bank[:].bitcast(BF16).rearrange("m (t p z e) -> m p t z e", t=PACK, z=2, e=2),
                )

        def pick_s(t, target, part):
            nc.vector.tensor_copy(target, s_raw[t][:].indirect(idx[:, entries(part)]))

        def sum_h(bank, t, part):
            for a in range(2):
                nc.tensor.matmul_mx(
                    out=bank,
                    lhsT=wk_w[a][:, P * t : P * (t + 1)].bitcast(E4M3),
                    lhsT_scale=wk_s[a][:, P * t : P * (t + 1)],
                    rhs=v_w[a][:, part].bitcast(E5M2),
                    rhs_scale=v_s[a][:, part],
                    start=(a == 0),
                    stop=(a == 1),
                )

        def empty_h(target, bank, t):
            nc.scalar.activation(target, bank, COPY, scale=minus_slope[:, t : t + 1])

        def first_factor(t, square):
            nc.scalar.activation(
                factor[:, t], square, IDENTITY, scale=minus_slope[:, t : t + 1], bias=slope_sb[:, t : t + 1]
            )

        def less_one(values):
            nc.scalar.activation(values, values, COPY, bias=-1.0, scale=1.0)

        def less_one_aside(values):
            nc.gpsimd.tensor_scalar(values, values, 1.0, -1.0, MULT, ADD)

        def first_d(k):
            nc.vector.tensor_tensor(
                d_in[0][:, PASS * k : PASS * (k + 1)].rearrange("p (c i e) -> p c e i", i=4, e=PACK),
                h_first[k][:].rearrange("p t (c i) -> p c t i", i=4),
                factor[:, :, P * k : P * (k + 1)].rearrange("p t (c i) -> p c t i", i=4),
                MULT,
            )

        def pair_d(j, t, h, values):
            n = 2 * width(PIECES[j])
            pairs = d_pairs[j][:, n * (t // 2) : n * (t // 2 + 1)].rearrange("p (c e) -> p c e", e=2)
            nc.gpsimd.tensor_tensor(pairs[:, :, t % 2], h, values, MULT)

        def lay_d(j):
            nc.scalar.copy(
                out=d_in[j][:].bitcast(F32).rearrange("p (c u) -> p c u", u=2),
                in_=d_pairs[j][:].bitcast(F32).rearrange("p (u c) -> p c u", u=2),
            )

        def quantise_d(j):
            part = PIECES[j]
            f = part.start // HALF
            inside = slice(part.start - f * HALF, part.stop - f * HALF)
            quantise(d_w[f][:, inside], d_s[f][:, inside], d_in[j][:])

        def open_y(b, part):
            acc = ps_y.tile([P, HALF], F32, name="acc")[:, 0 : width(part)]
            for a in range(2):
                nc.tensor.matmul_mx(
                    out=acc,
                    lhsT=c_w[a][:, P * b : P * (b + 1)].bitcast(E4M3),
                    lhsT_scale=c_s[:, a, P * b : P * (b + 1)],
                    rhs=v_w[a][:, part].bitcast(E5M2),
                    rhs_scale=v_s[a][:, part],
                    start=(a == 0),
                    stop=False,
                )
            return acc

        def close_y(b, part, acc):
            f = part.start // HALF
            inside = slice(part.start - f * HALF, part.stop - f * HALF)
            a, j = divmod(b, PACK)
            nc.tensor.matmul_mx(
                out=acc,
                lhsT=wr_w[a][:, P * j : P * (j + 1)].bitcast(E4M3),
                lhsT_scale=wr_s[a][:, P * j : P * (j + 1)],
                rhs=d_w[f][:, inside].bitcast(E4M3),
                rhs_scale=d_s[f][:, inside],
                start=False,
                stop=True,
            )
            return acc

        def sum_y(b, part):
            return close_y(b, part, open_y(b, part))

        def make_y(b, part, y):
            nc.scalar.activation(y, sum_y(b, part), COPY, scale=gain_sb[:, b : b + 1])

        def place(b, y, part):
            nc.vector.tensor_tensor(
                pages[b % PAGES][:].indirect(idx2[:, entries(part)]), y, wgo_sb[:, part], MULT
            )

        def store(b):
            nc.sync.dma_start(out=out[P * b : P * (b + 1), :], in_=pages[b % PAGES][:])

        pick_words(0, slice(0, S))
        pick_scales()
        for t in range(1, PACK):
            for part in (slice(0, T // 2), slice(T // 2, T)):
                load_s(t, part)
        nc.sync.dma_start(out=wgo_sb[:, PIECES[0]], in_=wgo[:, PIECES[0]])
        for q in range(4):
            nc.sync.dma_start(
                out=c_s[32 * q : 32 * q + 4, :, :].bitcast(I32),
                in_=c_scales.bitcast(I32)[:, 4 * q : 4 * q + 4, :].rearrange("a q n -> q a n"),
            )
        for f in range(2):
            for a in range(2):
                load_words(c_w[a], c_words[a], cols(f))
            if f == 0:
                nc.sync.dma_start(idx2[:], offs2)
        nc.sync.dma_start(out=wgo_sb[:, QUARTER:S], in_=wgo[:, QUARTER:S])
        lay_w(0, P // 2, lambda laid, raw: nc.gpsimd.tensor_scalar(laid, raw, 1.0, 0.0, MULT, ADD))
        quantise(wk_w[0][:], wk_s[0][:], wk_in[0][:])
        turn_w(0)
        pick_s(0, picked_first[:], slice(0, S))
        lay_w(1, 3 * P // 8, nc.vector.tensor_copy)
        wr_w = [held("wr_w0", [P, PASS], U32)]
        quantise(wr_w[0][:], wr_s[0][:], wr_in[0][:])
        quantise(wk_w[1][:], wk_s[1][:], wk_in[1][:])
        squares = held("w_raw1", [P, S], F32)
        for f in range(2):
            nc.scalar.activation(squares[:, cols(f)], picked[0][f], SQUARE)
        less_one_aside(squares[:, QUARTER:S])
        turn_w(1)
        for f in range(2):
            pick_words(1, cols(f))
        gain_bank = ps_h.tile([P, HALF], F32, name="h_rest1")
        nc.tensor.transpose(gain_bank[:, 0:P], gain_rows[:], ident[:])
        nc.scalar.copy(out=gain_sb[:], in_=gain_bank[:, 0 : N // P])
        h_rest.append(ps_h.tile([P, HALF], F32, name="h_rest1"))
        nc.scalar.activation(minus_slope[:], slope_sb[:], COPY, scale=-1.0)
        first_factor(0, squares[:, quarter(0)])
        bank = ps_y.tile([P, HALF], F32, name="acc")
        for t in range(2):
            sum_h(bank[:, quarter(t)], t, quarter(1))
        for t in range(2):
            empty_h(h_early[:, quarter(t)], bank[:, quarter(t)], t)
        pair_d(1, 0, h_early[:, quarter(0)], squares[:, quarter(1)])
        bank = ps_y.tile([P, HALF], F32, name="acc")
        sum_h(bank[:], 0, cols(1))
        empty_h(h_zero[:], bank[:], 0)
        pair_d(2, 0, h_zero[:], squares[:, cols(1)])
        for f in range(2):
            pick_s(1, picked[1][f], cols(f))
        nc.scalar.activation(early[:], picked[1][0], SQUARE)
        first_factor(1, early[:, quarter(0)])
        less_one_aside(early[:, quarter(1)])
        pair_d(1, 1, h_early[:, quarter(1)], early[:, quarter(1)])
        h_one = held("picked10", [P, HALF], F32)
        bank = ps_y.tile([P, HALF], F32, name="acc")
        sum_h(bank[:], 1, cols(1))
        empty_h(h_one[:], bank[:], 1)
        nc.scalar.activation(picked[1][1], picked[1][1], SQUARE)
        less_one_aside(picked[1][1])
        pair_d(2, 1, h_one[:], picked[1][1])
        for u in range(2):
            sum_h(h_second[:, quarter(u)], 2 + u, quarter(1))
        for k in range(2):
            for t in range(PACK):
                sum_h(h_first[k][:, t], t, slice(P * k, P * (k + 1)))
        for u in range(2):
            sum_h(h_rest[u][:], 2 + u, cols(1))
        for f in range(2):
            pick_s(2, third[f][:], cols(f))
        for k in range(3):
            pick_s(3, fourth[k][:], LAST_CUTS[k])
        nc.scalar.activation(third[0][:], third[0][:], SQUARE)
        first_factor(2, third[0][:, quarter(0)])
        less_one(third[0][:, quarter(1)])
        empty_h(h_two[:], h_second[:, quarter(0)], 2)
        pair_d(1, 2, h_two[:], third[0][:, quarter(1)])
        chain_square = held("chain_square", [P, QUARTER], F32)
        nc.scalar.activation(chain_square[:], fourth[0][:], SQUARE)
        first_factor(3, chain_square[:])
        for k in range(2):
            first_d(k)
        fourth.append(held("chain_square", [P, P], F32))
        pick_s(3, fourth[3][:], LAST_CUTS[3])
        behind = held("fourth0", [P, HALF + QUARTER], F32)
        h_three, third_rest = behind[:, quarter(0)], behind[:, QUARTER : QUARTER + HALF]
        empty_h(h_three, h_second[:, quarter(1)], 3)
        nc.scalar.activation(fourth[1][:], fourth[1][:], SQUARE)
        less_one(fourth[1][:])
        pair_d(1, 3, h_three, fourth[1][:])
        weight = held("weight", [P, QUARTER], F32)
        nc.scalar.activation(weight[:], wgo_sb[:, PIECES[0]], COPY, scale=gain_sb[:, 0:1])
        quantise_d(0)
        wr_w.append(held("factor", [P, PASS], U32))
        quantise(wr_w[1][:], wr_s[1][:], wr_in[1][:])
        nc.scalar.activation(third_rest, third[1][:], SQUARE)
        less_one(third_rest)
        lay_d(1)
        quantise_d(1)
        weighed = [held("weighed%d" % b, [P, QUARTER], F32) for b in range(PAGES)]
        opened = [open_y(b, PIECES[0]) for b in range(PAGES)]
        nc.vector.tensor_tensor(weighed[0][:], close_y(0, PIECES[0], opened[0]), weight[:], MULT)
        for b in range(1, PAGES):
            y = held("y_first%d" % b, [P, QUARTER], F32)
            nc.scalar.activation(y[:], close_y(b, PIECES[0], opened[b]), COPY, scale=gain_sb[:, b : b + 1])
            nc.gpsimd.tensor_tensor(weighed[b][:], y[:], wgo_sb[:, PIECES[0]], MULT)
        for b in range(PAGES):
            nc.vector.tensor_copy(pages[b][:].indirect(idx2[:, entries(PIECES[0])]), weighed[b][:])
        h_two_rest = held("y_first1", [P, HALF], F32)
        empty_h(h_two_rest[:], h_rest[0][:], 2)
        pair_d(2, 2, h_two_rest[:], third_rest)
        last = held("weight", [P, HALF], F32)
        for k in range(2):
            part = LAST_CUTS[2 + k]
            nc.scalar.activation(last[:, part.start - HALF : part.stop - HALF], fourth[2 + k][:], SQUARE)
        less_one(last[:])
        h_last = held("y_first2", [P, HALF], F32)
        empty_h(h_last[:], h_rest[1][:], 3)
        pair_d(2, 3, h_last[:], last[:])
        first = [yring.tile([P, S], F32, name="y") for b in range(PAGES)]
        make_y(0, PIECES[1], first[0][:, PIECES[1]])
        place(0, first[0][:, PIECES[1]], PIECES[1])
        lay_d(2)
        quantise_d(2)
        y_second = held("d_pairs2", [P, QUARTER], F32)
        make_y(1, PIECES[1], y_second[:])
        place(1, y_second[:], PIECES[1])
        for b in range(PAGES):
            parts = PIECES[2:] if b < COPIED else PIECES[1:]
            for part in parts:
                make_y(b, part, first[b][:, part])
            left = slice(parts[0].start, S)
            place(b, first[b][:, left], left)
            store(b)
        for b in range(PAGES, N // P):
            y = yring.tile([P, S], F32, name="y")
            for f in range(2):
                make_y(b, cols(f), y[:, cols(f)])
            place(b, y[:], slice(0, S))
            store(b)
